import numpy as np
import ml_dtypes


def mxq(x, axis, fmt="e4m3"):
    dtype, down = {"e4m3": (ml_dtypes.float8_e4m3fn, 7), "e5m2": (ml_dtypes.float8_e5m2, 14)}[fmt]
    v = np.moveaxis(np.asarray(x, np.float32).astype(ml_dtypes.bfloat16).astype(np.float64), axis, -1)
    blocks = v.reshape(v.shape[:-1] + (-1, 32))
    amax = np.abs(blocks).max(-1, keepdims=True)
    byte = np.maximum(np.where(amax > 0, np.frexp(amax)[1] - 1 + 127, 0) - down, 1)
    scale = np.exp2(byte - 127.0)
    codes = (blocks / scale).astype(np.float32).astype(dtype).astype(np.float64)
    return np.moveaxis((codes * scale).reshape(v.shape), -1, axis)


WIDE = False


def mx_kscale(k):
    if not WIDE:
        return np.ones(k)
    levels = np.array([10, -10, 5, -5, 0])
    if k % 512:
        return np.exp2(np.random.permutation(np.resize(levels, k // 32))).repeat(32)
    a = np.empty((k // 512, 16))
    for p in range(k // 512):
        a[p, :8] = np.random.permutation(np.resize(levels, 8))
        for g in range(8):
            far = levels[np.abs(levels - a[p, g]) >= 10]
            a[p, g + 8] = far[np.random.randint(len(far))]
    return np.exp2(a.ravel()).repeat(32)


def f64(x):
    return np.asarray(x).astype(np.float64)


def striped(idx):
    return np.tile(idx.reshape(-1, 16).T, (8, 1)).astype(np.uint16)


def unstriped(offs):
    return offs[:16].T.reshape(-1).astype(np.int64)


E2M1 = np.array([0.0, 0.5, 1.0, 1.5, 2.0, 3.0, 4.0, 6.0, -0.0, -0.5, -1.0, -1.5, -2.0, -3.0, -4.0, -6.0])


def pack_weight(w, fmt):
    k, n = w.shape
    w = f64(np.asarray(w, np.float32).astype(ml_dtypes.bfloat16)).reshape(k // 32, 32, n)
    amax = np.abs(w).max(1)
    if fmt == "e4m3":
        byte = np.frexp(amax)[1] - 1 + 127 - 7
    else:
        mant, ex = np.frexp(amax / 6.0)
        byte = np.where(mant > 0.5, ex, ex - 1) + 127
    byte = np.clip(np.where(amax > 0, byte, 1), 1, 254)
    scaled = (w * np.exp2(127.0 - byte)[:, None, :]).reshape(k, n).astype(np.float32)
    by_word = np.ascontiguousarray(scaled.reshape(k // 512, 128, 4, n).transpose(0, 1, 3, 2))
    if fmt == "e4m3":
        words = by_word.astype(ml_dtypes.float8_e4m3fn).view(np.uint8)
    else:
        c = by_word.astype(ml_dtypes.float4_e2m1fn).view(np.uint8) & 0xF
        words = (c[..., 0::2] | (c[..., 1::2] << 4)).reshape(k // 512, 128, 2 * n)
    return np.ascontiguousarray(words), np.ascontiguousarray(byte.astype(np.uint8).reshape(k // 512, 16, n))


def unpack_weight(words, scales, fmt):
    g, _, n = scales.shape
    words = np.ascontiguousarray(words).reshape(g, 128, n, -1)
    if fmt == "e4m3":
        vals = words.view(ml_dtypes.float8_e4m3fn).astype(np.float64)
    else:
        nib = np.empty((g, 128, n, 4), np.uint8)
        nib[..., 0::2] = words & 0xF
        nib[..., 1::2] = words >> 4
        vals = E2M1[nib]
    vals = vals * np.repeat(np.exp2(scales.astype(np.float64) - 127.0), 8, axis=1)[..., None]
    return vals.transpose(0, 1, 3, 2).reshape(g * 512, n)


def gelu(v):
    return 0.5 * v * (1.0 + np.tanh(np.sqrt(2.0 / np.pi) * (v + 0.044715 * v**3)))


K, K2, T, S, H, T2, P, N = 1024, 512, 2048, 512, 1024, 2048, 1024, 512

def setup_inputs():
    n = np.random.standard_normal
    s, s2, u = mx_kscale(K)[:, None], mx_kscale(K2)[:, None], mx_kscale(H)[:, None]
    perm = np.random.permutation(T2)
    d = {}
    d["tab_words"], d["tab_scales"] = pack_weight(n((K, T)) * s, "e4m3")
    d["tab2_words"], d["tab2_scales"] = pack_weight(n((K2, T)) * s2, "e4m3")
    d["offs"] = striped(np.random.permutation(T)[:S])
    d["offs2"] = striped(np.random.permutation(T)[:S])
    d["offs3"] = striped(perm[:S])
    d["offs4"] = striped(perm[S:2 * S])
    d["offs5"] = striped(np.random.permutation(T2)[:P])
    d["w1"] = (n((K, H)) * 0.52 / K**0.5 / s).astype(np.float32)
    d["amp"] = (2.0 * np.exp(0.3 * n(H)) * u[:, 0]).astype(np.float32)
    d["w2_words"], d["w2_scales"] = pack_weight(n((K2, H)) * 0.9 / K2**0.5 / s2 * u.T, "e2m1")
    d["coup"] = n((H, S)).astype(np.float32)
    d["w3"] = (n((K2, H)) * 0.9 / K2**0.5 / s2 * u.T).astype(np.float32)
    d["page0"] = (n((H, T2)) * u).astype(np.float32)
    d["wg1"] = np.exp(0.3 * n((128, S))).astype(np.float32)
    d["wg2"] = np.exp(0.3 * n((128, S))).astype(np.float32)
    d["gain"] = np.exp(0.4 * n(H)).astype(np.float32)
    d["w4_words"], d["w4_scales"] = pack_weight(n((H, N)) * 0.8 / H**0.5 / u, "e4m3")
    d["bias"] = (0.8 * n(N)).astype(np.float32)
    return d

def reference(tab_words, tab_scales, tab2_words, tab2_scales, offs, offs2, offs3, offs4, offs5, w1, amp, w2_words, w2_scales, coup, w3, page0, wg1, wg2, gain, w4_words, w4_scales, bias):
    v = unpack_weight(tab_words, tab_scales, "e4m3")[:, unstriped(offs)]
    v2 = unpack_weight(tab2_words, tab2_scales, "e4m3")[:, unstriped(offs2)]
    w2 = unpack_weight(w2_words, w2_scales, "e2m1")
    w4 = unpack_weight(w4_words, w4_scales, "e4m3")
    h1 = f64(amp)[:, None] * np.cos(mxq(f64(w1), 0, "e4m3").T @ v)
    h2 = (w2.T @ v2) * f64(coup) + (mxq(f64(w3), 0, "e4m3").T @ v2)
    page = f64(page0).copy()
    page[:, unstriped(offs3)] = np.tile(f64(wg1), (H // 128, 1)) * h1
    page[:, unstriped(offs4)] = np.tile(f64(wg2), (H // 128, 1)) * h2
    x = page[:, unstriped(offs5)] * f64(gain)[:, None]
    y = (w4.T @ mxq(x, 0, "e4m3")) + f64(bias)[:, None]
    return np.abs(y)

@@ -1,0 +1,386 @@
+from contextlib import ExitStack
+
+import concourse.mybir as mybir
+
+F32 = mybir.dt.float32
+BF16 = mybir.dt.bfloat16
+I32 = mybir.dt.int32
+U32 = mybir.dt.uint32
+U16 = mybir.dt.uint16
+U8 = mybir.dt.uint8
+FP8X4 = mybir.dt.float8_e4m3fn_x4
+FP4X4 = mybir.dt.float4_e2m1fn_x4
+ACT = mybir.ActivationFunctionType
+MULT = mybir.AluOpType.mult
+ADD = mybir.AluOpType.add
+
+K, K2, T, S, H, T2, NP, N = 1024, 512, 2048, 512, 1024, 2048, 1024, 512
+FLOPS = 2 * K * H * S + 2 * 2 * K2 * H * S + 2 * H * N * NP
+
+P = 128
+PACK = 4
+KP = P * PACK
+CHUNKS = [(0, 256), (256, 256), (512, 256), (768, 128), (896, 128)]
+
+
+def tile_list_glitch_catalogue_read_kernel(
+    tc, tab_words, tab_scales, tab2_words, tab2_scales, offs, offs2, offs3, offs4, offs5,
+    w1, amp, w2_words, w2_scales, coup, w3, page0, wg1, wg2, gain, w4_words, w4_scales, bias, out,
+):
+    nc = tc.nc
+    with ExitStack() as ctx:
+        held = ctx.enter_context(tc.tile_pool(name="held", bufs=1))
+        ring = ctx.enter_context(tc.tile_pool(name="ring", bufs=2))
+        psum = ctx.enter_context(tc.psum_pool(name="psum", bufs=1))
+
+        def keep(shape, dtype, name):
+            return held.tile(shape, dtype, name=name, align_bytes=64)
+
+        def turn(shape, dtype, tag, bufs, name):
+            return ring.tile(shape, dtype, tag=tag, bufs=bufs, name=name, align_bytes=64)
+
+        banks = [psum.tile([P, 512], F32, name=f"bank{i}") for i in range(8)]
+
+        lists = {}
+
+        def load_list(name, src):
+            lists[name] = keep(list(src.shape), U16, name + "_t")
+            nc.sync.dma_start(lists[name][:], src)
+
+        def scale_tile(name, width):
+            plane = keep([P, width], U8, name)
+            nc.vector.memset(plane[:].bitcast(I32), 0)
+            return plane
+
+        def load_scales(plane, src):
+            rows = PACK * src.shape[0]
+            for q in range(4):
+                nc.sync.dma_start(plane[32 * q : 32 * q + rows, :].bitcast(I32), src[:, 4 * q : 4 * q + 4, :].bitcast(I32))
+
+        def load_words(name, src):
+            words = turn([P, src.shape[1]], I32, "table", 3, name) if src.shape[1] == T else keep([P, src.shape[1]], I32, name)
+            nc.sync.dma_start(words[:], src.rearrange("p n i -> p (n i)").bitcast(I32))
+            return words
+
+        def load_weight(name, w, a, b):
+            raw = turn([P, PACK, KP], F32, "wraw", 6, name)
+            nc.sync.dma_start(raw[:], w[KP * a : KP * (a + 1), KP * b : KP * (b + 1)].rearrange("(p j) c -> p j c", j=PACK))
+            return raw
+
+        def rows_of(x, b, t):
+            return x[KP * b : KP * (b + 1), :].rearrange("(p t) c -> p t c", t=PACK)[:, t, :]
+
+        coup_t, page_t, coup_pair = {}, {}, {}
+
+        def load_coup(b, t0, count):
+            rows = turn([P, 2, S], F32, "coup", 2, f"coup{b}{t0}") if t0 % 2 == 0 else coup_pair[0]
+            coup_pair[0] = rows
+            src = coup[KP * b : KP * (b + 1), :].rearrange("(p t) c -> p t c", t=PACK)
+            nc.sync.dma_start(rows[:, t0 % 2 : t0 % 2 + count, :], src[:, t0 : t0 + count, :])
+            for t in range(t0, t0 + count):
+                coup_t[b, t] = rows[:, t % 2, :]
+
+        def load_page(b, t):
+            page_t[b, t] = turn([P, T2], F32, "page", 4, f"page{b}{t}")
+            nc.sync.dma_start(page_t[b, t][:], rows_of(page0, b, t))
+
+        wg_t = {}
+
+        wg_pair = {}
+
+        def load_wg(name, src, t0, t1):
+            if t0 % 2 == 0:
+                wg_pair[name, t0] = keep([P, 2, S], F32, f"{name}_{t0}")
+            dealt = wg_pair[name, t0 - t0 % 2]
+            for q in range(4):
+                nc.sync.dma_start(dealt[32 * q : 32 * (q + 1), t0 % 2 : t0 % 2 + t1 - t0, :], src.rearrange("(p t) c -> p t c", t=PACK)[:, t0:t1, :])
+            for t in range(t0, t1):
+                wg_t[name, t] = dealt[:, t % 2, :]
+
+        def load_rowvec(name, src):
+            vec = keep([P, 2, PACK], F32, name)
+            nc.sync.dma_start(vec[:], src.rearrange("(b p t) -> p b t", b=2, t=PACK))
+            return vec
+
+        tab2_plane = scale_tile("tab2_plane", T)
+        w2_plane_raw = scale_tile("w2_plane_raw", H)
+        tab_plane = scale_tile("tab_plane", T)
+        w4_plane = scale_tile("w4_plane", N)
+
+        raws = {}
+        load_list("offs2", offs2)
+        tab2_w = load_words("tab2_w", tab2_words[0])
+        load_scales(tab2_plane, tab2_scales)
+        raws["w3", 0, 0] = load_weight("w3_00", w3, 0, 0)
+        w2_raw = keep([P, 2 * H], U8, "w2_raw")
+        nc.sync.dma_start(w2_raw[:].bitcast(I32), w2_words[0].bitcast(I32))
+        load_scales(w2_plane_raw, w2_scales)
+        load_coup(0, 0, 1)
+        load_page(0, 0)
+        load_wg("wg2", wg2, 0, 1)
+        load_list("offs4", offs4)
+        load_list("offs", offs)
+        tab_w = [load_words(f"tab_w{a}", tab_words[a]) for a in range(2)]
+        load_scales(tab_plane, tab_scales)
+        raws["w1", 0, 0] = load_weight("w1_00", w1, 0, 0)
+        raws["w1", 1, 0] = load_weight("w1_10", w1, 1, 0)
+        amp_t = load_rowvec("amp_t", amp)
+        load_coup(0, 1, 1)
+        load_wg("wg2", wg2, 1, 2)
+        load_page(0, 1)
+        load_wg("wg1", wg1, 0, 2)
+        load_list("offs3", offs3)
+        load_list("offs5", offs5)
+        load_coup(0, 2, 2)
+        load_wg("wg2", wg2, 2, 4)
+        raws["w3", 0, 1] = load_weight("w3_01", w3, 0, 1)
+        load_wg("wg1", wg1, 2, 4)
+        raws["w1", 0, 1] = load_weight("w1_01", w1, 0, 1)
+        raws["w1", 1, 1] = load_weight("w1_11", w1, 1, 1)
+        gain_t = load_rowvec("gain_t", gain)
+        load_page(0, 2)
+        load_page(0, 3)
+        load_coup(1, 0, 2)
+        load_page(1, 0)
+        load_page(1, 1)
+        w4_w = [load_words(f"w4_w{a}", w4_words[a]) for a in range(2)]
+        load_scales(w4_plane, w4_scales)
+        bias_t = keep([P, 4], F32, "bias_t")
+        with nc.allow_non_contiguous_dma(reason="one bias value for each output row"):
+            nc.sync.dma_start(bias_t[:], bias.rearrange("(n p) -> p n", p=P))
+        load_page(1, 2)
+        load_page(1, 3)
+        load_coup(1, 2, 2)
+
+        def gather_words(name, words, lst):
+            picked = keep([P, S], U32, name)
+            nc.vector.tensor_copy(picked[:], words[:].bitcast(U32).indirect(lists[lst][:]))
+            return picked
+
+        def gather_plane(name, plane, lst):
+            picked = keep([P, S], U8, name)
+            nc.vector.tensor_copy(picked[:], plane[:].indirect(lists[lst][:]))
+            return picked
+
+        codes, planes = {}, {}
+
+        def quantise_weight(key, split):
+            raw = raws[key]
+            name = "%s_%d%d" % key
+            rounded = turn([P, PACK * KP], BF16, "wbf", 3, name + "_bf")
+            dst = rounded[:].rearrange("p (t m j) -> p m j t", t=PACK, j=PACK)
+            src = raw[:].rearrange("p j (m t) -> p m j t", t=PACK)
+            if split:
+                nc.scalar.copy(dst[:, :split], src[:, :split])
+                nc.vector.tensor_copy(dst[:, split:], src[:, split:])
+            else:
+                nc.scalar.copy(dst, src)
+            codes[key] = keep([P, KP], U32, name + "_codes")
+            planes[key] = keep([P, KP], U8, name + "_plane")
+            nc.vector.quantize_mx(out=codes[key][:].bitcast(FP8X4), scales=planes[key][:], in_=rounded[:])
+
+        v2_w = gather_words("v2_w", tab2_w, "offs2")
+        v2_plane = gather_plane("v2_plane", tab2_plane, "offs2")
+        quantise_weight(("w3", 0, 0), 64)
+
+        w2_dealt = keep([P, 2 * H], U8, "w2_dealt")
+        w2_plane = keep([P, H], U8, "w2_plane")
+        for b in range(2):
+            nc.vector.tensor_copy(
+                w2_dealt[:, 2 * KP * b : 2 * KP * (b + 1)].rearrange("p (t m e) -> p m t e", t=PACK, e=2),
+                w2_raw[:, 2 * KP * b : 2 * KP * (b + 1)].rearrange("p (m t e) -> p m t e", t=PACK, e=2),
+            )
+            nc.vector.tensor_copy(
+                w2_plane[:, KP * b : KP * (b + 1)].rearrange("p (t m) -> p m t", t=PACK),
+                w2_plane_raw[:, KP * b : KP * (b + 1)].rearrange("p (m t) -> p m t", t=PACK),
+            )
+
+        used = []
+
+        def next_bank():
+            used.append(None)
+            return banks[4 + (len(used) - 1) % 4]
+
+        def products2(b, t, bank_a, bank_b):
+            cols = slice(P * t, P * (t + 1))
+            c0 = KP * b + P * t
+            nc.tensor.matmul_mx(
+                out=bank_a[:], lhsT=w2_dealt[:, 2 * c0 : 2 * (c0 + P)].bitcast(FP4X4), lhsT_scale=w2_plane[:, c0 : c0 + P],
+                rhs=v2_w[:].bitcast(FP8X4), rhs_scale=v2_plane[:], start=True, stop=True,
+            )
+            nc.tensor.matmul_mx(
+                out=bank_b[:], lhsT=codes["w3", 0, b][:, cols].bitcast(FP8X4), lhsT_scale=planes["w3", 0, b][:, cols],
+                rhs=v2_w[:].bitcast(FP8X4), rhs_scale=v2_plane[:], start=True, stop=True,
+            )
+            return bank_a, bank_b
+
+        def cosine(b, t, h1):
+            cols = slice(P * t, P * (t + 1))
+            bank = next_bank()
+            for a in range(2):
+                nc.tensor.matmul_mx(
+                    out=bank[:], lhsT=codes["w1", a, b][:, cols].bitcast(FP8X4), lhsT_scale=planes["w1", a, b][:, cols],
+                    rhs=v_w[a][:].bitcast(FP8X4), rhs_scale=v_plane[PACK * a : P, :], start=(a == 0), stop=(a == 1),
+                )
+            nc.scalar.activation(h1, bank[:], ACT.Sin, scale=0.5)
+            nc.scalar.activation(h1, h1, ACT.Square)
+            nc.scalar.activation(h1, h1, ACT.Identity, bias=amp_t[:, b, t : t + 1], scale=amp_m2[:, b, t : t + 1])
+
+        def window(b, t, lst):
+            return page_t[b, t][:].indirect(lists[lst][:])
+
+        h2_first = turn([P, 2, S], F32, "h2", 3, "h2_first")
+
+        def first2(t):
+            bank_a, bank_b = products2(0, t, banks[2 * t], banks[2 * t + 1])
+            h2 = h2_first[:, t, :]
+            nc.vector.tensor_tensor(h2, bank_a[:], coup_t[0, t], MULT)
+            nc.vector.tensor_tensor(h2, bank_b[:], h2, ADD)
+            nc.vector.tensor_tensor(window(0, t, "offs4"), h2, wg_t["wg2", t], MULT)
+
+        def first1():
+            h1 = turn([P, 2, S], F32, "h1", 3, "h1_first")
+            for t in range(2):
+                cosine(0, t, h1[:, t, :])
+            return [lambda t=t: nc.vector.tensor_tensor(window(0, t, "offs3"), h1[:, t, :], wg_t["wg1", t], MULT) for t in range(2)]
+
+        def stream2(b, t0):
+            h2 = turn([P, 2, S], F32, *(("last", 2) if (b, t0) == (1, 2) else ("h2", 3)), f"h2_{b}{t0}")
+            plain = turn([P, 2, S], F32, "plain", 2, f"plain_{b}{t0}")
+            for u in range(2):
+                bank_a, bank_b = products2(b, t0 + u, next_bank(), next_bank())
+                nc.scalar.copy(h2[:, u, :], bank_a[:])
+                nc.scalar.copy(plain[:, u, :], bank_b[:])
+                nc.gpsimd.tensor_tensor(h2[:, u, :], h2[:, u, :], coup_t[b, t0 + u], MULT)
+                nc.gpsimd.tensor_tensor(h2[:, u, :], h2[:, u, :], plain[:, u, :], ADD)
+            nc.gpsimd.tensor_tensor(h2[:], h2[:], wg_pair["wg2", t0][:], MULT)
+            return [lambda u=u: nc.vector.tensor_copy(window(b, t0 + u, "offs4"), h2[:, u, :]) for u in range(2)]
+
+        def stream1(b, t0):
+            h1 = turn([P, 2, S], F32, *(("last", 2) if (b, t0) == (1, 2) else ("h1", 3)), f"h1_{b}{t0}")
+            for u in range(2):
+                cosine(b, t0 + u, h1[:, u, :])
+            nc.gpsimd.tensor_tensor(h1[:], h1[:], wg_pair["wg1", t0][:], MULT)
+            return [lambda u=u: nc.vector.tensor_copy(window(b, t0 + u, "offs3"), h1[:, u, :]) for u in range(2)]
+
+        first2(0)
+        v_w = [gather_words(f"v_w{a}", tab_w[a], "offs") for a in range(2)]
+        v_plane = gather_plane("v_plane", tab_plane, "offs")
+        quantise_weight(("w1", 0, 0), 0)
+        quantise_weight(("w1", 1, 0), 64)
+        amp_m2 = keep([P, 2, PACK], F32, "amp_m2")
+        nc.vector.tensor_scalar(amp_m2[:], amp_t[:], -2.0, None, MULT)
+
+        x0_rows = turn([P, PACK, NP], BF16, "table", 3, "x0_rows")
+
+        def fetch0(t):
+            got = turn([P, NP], F32, "got", 3, f"got0{t}")
+            nc.vector.tensor_copy(got[:], page_t[0, t][:].indirect(lists["offs5"][:]))
+            nc.scalar.activation(x0_rows[:, t, :], got[:], ACT.Copy, scale=gain_t[:, 0, t : t + 1])
+
+        x0_codes = keep([P, NP], U32, "x0_codes")
+        x0_plane = keep([P, NP], U8, "x0_plane")
+
+        def quantise_x0(h):
+            cols = slice(512 * h, 512 * (h + 1))
+            woven = turn([P, PACK * 512], BF16, "table", 3, f"woven0{h}")
+            nc.scalar.copy(
+                woven[:].rearrange("p (c i t) -> p c t i", i=4, t=PACK),
+                x0_rows[:, :, cols].rearrange("p t (c i) -> p c t i", i=4),
+            )
+            nc.vector.quantize_mx(out=x0_codes[:, cols].bitcast(FP8X4), scales=x0_plane[:, cols], in_=woven[:])
+
+        woven1 = turn([P, PACK * NP], BF16, "wraw", 6, "woven1")
+        woven1_rows = woven1[:].rearrange("p (c t) -> p c t", t=PACK)
+
+        def fetch1_whole(t):
+            got = turn([P, NP], F32, "got", 3, f"got1{t}")
+            nc.vector.tensor_copy(got[:], window(1, t, "offs5"))
+            nc.scalar.activation(woven1_rows[:, :, t], got[:], ACT.Copy, scale=gain_t[:, 1, t : t + 1])
+
+        put1 = first1()
+        first2(1)
+        put1[0]()
+        put1[1]()
+        put2 = stream2(0, 2)
+        quantise_weight(("w3", 0, 1), 0)
+        put1 = stream1(0, 2)
+        quantise_weight(("w1", 0, 1), 0)
+        quantise_weight(("w1", 1, 1), 0)
+        fetch0(0)
+        fetch0(1)
+        for b, t0 in ((1, 0), (1, 2)):
+            next2, next1 = stream2(b, t0), stream1(b, t0)
+            put2[0]()
+            put1[0]()
+            put2[1]()
+            put1[1]()
+            put2, put1 = next2, next1
+            if t0 == 0:
+                fetch0(2)
+                fetch0(3)
+            else:
+                quantise_x0(0)
+                quantise_x0(1)
+                fetch1_whole(0)
+                fetch1_whole(1)
+        put1[0]()
+        put1[1]()
+
+        free_banks = list(banks)
+
+        def places(width):
+            per_bank = 512 // width
+            spots = []
+            for n in range(4):
+                if n % per_bank == 0:
+                    bank = free_banks.pop(0)
+                spots.append((bank[:, width * (n % per_bank) : width * (n % per_bank + 1)], n % per_bank == 0, n % per_bank == per_bank - 1))
+            return spots
+
+        def last_pass(a, spots, x_codes, x_plane):
+            for n, (place, first, last) in enumerate(spots):
+                cols = slice(P * n, P * (n + 1))
+                nc.tensor.matmul_mx(
+                    out=place, lhsT=w4_w[a][:, cols].bitcast(FP8X4), lhsT_scale=w4_plane[PACK * a : P, cols],
+                    rhs=x_codes.bitcast(FP8X4), rhs_scale=x_plane, start=(a == 0 and first), stop=(a == 1 and last),
+                )
+
+        sums = []
+        for c0, width in CHUNKS:
+            sums.append(places(width))
+            last_pass(0, sums[-1], x0_codes[:, c0 : c0 + width], x0_plane[:, c0 : c0 + width])
+        put2[0]()
+        put2[1]()
+
+        out_rows = out.rearrange("(n p) j -> p n j", p=P)
+
+        def fetch1(i):
+            c0, width = CHUNKS[i]
+            got = turn([P, 2, 256], F32, "last", 2, f"got_last{i}")
+            for u in range(2):
+                nc.vector.tensor_copy(got[:, u, :width], page_t[1, 2 + u][:].indirect(lists["offs5"][:, c0 // 16 : (c0 + width) // 16]))
+            engine = nc.vector if i == len(CHUNKS) - 1 else nc.gpsimd
+            engine.tensor_tensor(
+                woven1_rows[:, c0 : c0 + width, 2:4], got[:, :, :width].rearrange("p u c -> p c u"),
+                gain_t[:, 1:2, 2:4].to_broadcast([P, width, 2]), MULT,
+            )
+
+        results = [turn([P, 4, 512], F32, "wraw", 6, f"result{h}") for h in range(2)]
+
+        def finish(i):
+            c0, width = CHUNKS[i]
+            x_codes = turn([P, 256], U32, "x1_codes", 2, f"x1_codes{i}")
+            x_plane = turn([P, 256], U8, "x1_plane", 2, f"x1_plane{i}")
+            nc.vector.quantize_mx(out=x_codes[:, :width].bitcast(FP8X4), scales=x_plane[:, :width], in_=woven1[:, PACK * c0 : PACK * (c0 + width)])
+            last_pass(1, sums[i], x_codes[:, :width], x_plane[:, :width])
+            result = results[c0 // 512][:, :, c0 % 512 : c0 % 512 + width]
+            for n, spot in enumerate(sums[i]):
+                nc.scalar.activation(result[:, n, :], spot[0], ACT.Abs, bias=bias_t[:, n : n + 1])
+            nc.sync.dma_start(out_rows[:, :, c0 : c0 + width], result)
+
+        for i in range(len(CHUNKS)):
+            fetch1(i)
+            if i > 0:
+                finish(i - 1)
+        finish(len(CHUNKS) - 1)

@@ -20,6 +20,7 @@ FLOPS = 2 * K * H * S + 2 * 2 * K2 * H * S + 2 * H * N * NP
 P = 128
 PACK = 4
 KP = P * PACK
+QUADRANTS = (0, 2, 1, 3)
 CHUNKS = [(0, 256), (256, 256), (512, 256), (768, 128), (896, 128)]
 
 
@@ -54,7 +55,7 @@ def tile_list_glitch_catalogue_read_kernel(
 
         def load_scales(plane, src):
             rows = PACK * src.shape[0]
-            for q in range(4):
+            for q in QUADRANTS:
                 nc.sync.dma_start(plane[32 * q : 32 * q + rows, :].bitcast(I32), src[:, 4 * q : 4 * q + 4, :].bitcast(I32))
 
         def load_words(name, src):
@@ -92,7 +93,7 @@ def tile_list_glitch_catalogue_read_kernel(
             if t0 % 2 == 0:
                 wg_pair[name, t0] = keep([P, 2, S], F32, f"{name}_{t0}")
             dealt = wg_pair[name, t0 - t0 % 2]
-            for q in range(4):
+            for q in QUADRANTS:
                 nc.sync.dma_start(dealt[32 * q : 32 * (q + 1), t0 % 2 : t0 % 2 + t1 - t0, :], src.rearrange("(p t) c -> p t c", t=PACK)[:, t0:t1, :])
             for t in range(t0, t1):
                 wg_t[name, t] = dealt[:, t % 2, :]
@@ -128,19 +129,20 @@ def tile_list_glitch_catalogue_read_kernel(
         load_coup(0, 1, 1)
         load_wg("wg2", wg2, 1, 2)
         load_page(0, 1)
-        load_wg("wg1", wg1, 0, 2)
+        load_wg("wg1", wg1, 0, 1)
         load_list("offs3", offs3)
         load_list("offs5", offs5)
+        load_wg("wg1", wg1, 1, 2)
         load_coup(0, 2, 2)
         load_wg("wg2", wg2, 2, 4)
-        raws["w3", 0, 1] = load_weight("w3_01", w3, 0, 1)
         load_wg("wg1", wg1, 2, 4)
+        raws["w3", 0, 1] = load_weight("w3_01", w3, 0, 1)
+        load_page(0, 2)
         raws["w1", 0, 1] = load_weight("w1_01", w1, 0, 1)
         raws["w1", 1, 1] = load_weight("w1_11", w1, 1, 1)
         gain_t = load_rowvec("gain_t", gain)
-        load_page(0, 2)
-        load_page(0, 3)
         load_coup(1, 0, 2)
+        load_page(0, 3)
         load_page(1, 0)
         load_page(1, 1)
         w4_w = [load_words(f"w4_w{a}", w4_words[a]) for a in range(2)]
@@ -229,39 +231,42 @@ def tile_list_glitch_catalogue_read_kernel(
         def window(b, t, lst):
             return page_t[b, t][:].indirect(lists[lst][:])
 
-        h2_first = turn([P, 2, S], F32, "h2", 3, "h2_first")
+        pairs = {}
+
+        def values(stream, b, t):
+            if t % 2 == 0:
+                tag, bufs = ("last", 2) if (b, t) == (1, 2) else (stream, 3)
+                pairs[stream] = turn([P, 2, S], F32, tag, bufs, f"{stream}_{b}{t}")
+            return pairs[stream][:, t % 2, :]
 
         def first2(t):
+            h2 = values("h2", 0, t)
             bank_a, bank_b = products2(0, t, banks[2 * t], banks[2 * t + 1])
-            h2 = h2_first[:, t, :]
             nc.vector.tensor_tensor(h2, bank_a[:], coup_t[0, t], MULT)
             nc.vector.tensor_tensor(h2, bank_b[:], h2, ADD)
             nc.vector.tensor_tensor(window(0, t, "offs4"), h2, wg_t["wg2", t], MULT)
 
         def first1():
-            h1 = turn([P, 2, S], F32, "h1", 3, "h1_first")
-            for t in range(2):
-                cosine(0, t, h1[:, t, :])
-            return [lambda t=t: nc.vector.tensor_tensor(window(0, t, "offs3"), h1[:, t, :], wg_t["wg1", t], MULT) for t in range(2)]
+            h1 = values("h1", 0, 0)
+            cosine(0, 0, h1)
+            return lambda: nc.vector.tensor_tensor(window(0, 0, "offs3"), h1, wg_t["wg1", 0], MULT)
 
-        def stream2(b, t0):
-            h2 = turn([P, 2, S], F32, *(("last", 2) if (b, t0) == (1, 2) else ("h2", 3)), f"h2_{b}{t0}")
-            plain = turn([P, 2, S], F32, "plain", 2, f"plain_{b}{t0}")
-            for u in range(2):
-                bank_a, bank_b = products2(b, t0 + u, next_bank(), next_bank())
-                nc.scalar.copy(h2[:, u, :], bank_a[:])
-                nc.scalar.copy(plain[:, u, :], bank_b[:])
-                nc.gpsimd.tensor_tensor(h2[:, u, :], h2[:, u, :], coup_t[b, t0 + u], MULT)
-                nc.gpsimd.tensor_tensor(h2[:, u, :], h2[:, u, :], plain[:, u, :], ADD)
-            nc.gpsimd.tensor_tensor(h2[:], h2[:], wg_pair["wg2", t0][:], MULT)
-            return [lambda u=u: nc.vector.tensor_copy(window(b, t0 + u, "offs4"), h2[:, u, :]) for u in range(2)]
+        def stream2(b, t):
+            h2 = values("h2", b, t)
+            plain = turn([P, S], F32, "plain", 2, f"plain_{b}{t}")
+            bank_a, bank_b = products2(b, t, next_bank(), next_bank())
+            nc.scalar.copy(h2, bank_a[:])
+            nc.scalar.copy(plain[:], bank_b[:])
+            nc.gpsimd.tensor_tensor(h2, h2, coup_t[b, t], MULT)
+            nc.gpsimd.tensor_tensor(h2, h2, plain[:], ADD)
+            nc.gpsimd.tensor_tensor(h2, h2, wg_t["wg2", t], MULT)
+            return lambda: nc.vector.tensor_copy(window(b, t, "offs4"), h2)
 
-        def stream1(b, t0):
-            h1 = turn([P, 2, S], F32, *(("last", 2) if (b, t0) == (1, 2) else ("h1", 3)), f"h1_{b}{t0}")
-            for u in range(2):
-                cosine(b, t0 + u, h1[:, u, :])
-            nc.gpsimd.tensor_tensor(h1[:], h1[:], wg_pair["wg1", t0][:], MULT)
-            return [lambda u=u: nc.vector.tensor_copy(window(b, t0 + u, "offs3"), h1[:, u, :]) for u in range(2)]
+        def stream1(b, t):
+            h1 = values("h1", b, t)
+            cosine(b, t, h1)
+            nc.gpsimd.tensor_tensor(h1, h1, wg_t["wg1", t], MULT)
+            return lambda: nc.vector.tensor_copy(window(b, t, "offs3"), h1)
 
         first2(0)
         v_w = [gather_words(f"v_w{a}", tab_w[a], "offs") for a in range(2)]
@@ -290,42 +295,39 @@ def tile_list_glitch_catalogue_read_kernel(
             )
             nc.vector.quantize_mx(out=x0_codes[:, cols].bitcast(FP8X4), scales=x0_plane[:, cols], in_=woven[:])
 
-        woven1 = turn([P, PACK * NP], BF16, "wraw", 6, "woven1")
-        woven1_rows = woven1[:].rearrange("p (c t) -> p c t", t=PACK)
+        x1_rows = turn([P, PACK, NP], BF16, "wraw", 6, "x1_rows")
 
         def fetch1_whole(t):
             got = turn([P, NP], F32, "got", 3, f"got1{t}")
             nc.vector.tensor_copy(got[:], window(1, t, "offs5"))
-            nc.scalar.activation(woven1_rows[:, :, t], got[:], ACT.Copy, scale=gain_t[:, 1, t : t + 1])
+            nc.scalar.activation(x1_rows[:, t, :], got[:], ACT.Copy, scale=gain_t[:, 1, t : t + 1])
 
-        put1 = first1()
+        put1, put2 = {(0, 0): first1(), (0, 1): stream1(0, 1)}, {}
         first2(1)
-        put1[0]()
-        put1[1]()
-        put2 = stream2(0, 2)
+        put1[0, 0]()
+        fetch0(0)
+        put1[0, 1]()
+        for t in (2, 3):
+            put2[0, t], put1[0, t] = stream2(0, t), stream1(0, t)
+        fetch0(1)
         quantise_weight(("w3", 0, 1), 0)
-        put1 = stream1(0, 2)
+        put2[0, 2]()
+        put1[0, 2]()
+        fetch0(2)
         quantise_weight(("w1", 0, 1), 0)
         quantise_weight(("w1", 1, 1), 0)
-        fetch0(0)
-        fetch0(1)
-        for b, t0 in ((1, 0), (1, 2)):
-            next2, next1 = stream2(b, t0), stream1(b, t0)
-            put2[0]()
-            put1[0]()
-            put2[1]()
-            put1[1]()
-            put2, put1 = next2, next1
-            if t0 == 0:
-                fetch0(2)
-                fetch0(3)
-            else:
-                quantise_x0(0)
-                quantise_x0(1)
-                fetch1_whole(0)
-                fetch1_whole(1)
-        put1[0]()
-        put1[1]()
+        put2[0, 3]()
+        put1[0, 3]()
+        for t in range(PACK):
+            put2[1, t], put1[1, t] = stream2(1, t), stream1(1, t)
+        fetch0(3)
+        for t in range(2):
+            put2[1, t]()
+            put1[1, t]()
+            quantise_x0(t)
+            fetch1_whole(t)
+        put2[1, 2]()
+        put2[1, 3]()
 
         free_banks = list(banks)
 
@@ -350,37 +352,52 @@ def tile_list_glitch_catalogue_read_kernel(
         for c0, width in CHUNKS:
             sums.append(places(width))
             last_pass(0, sums[-1], x0_codes[:, c0 : c0 + width], x0_plane[:, c0 : c0 + width])
-        put2[0]()
-        put2[1]()
+        put1[1, 2]()
+        put1[1, 3]()
 
         out_rows = out.rearrange("(n p) j -> p n j", p=P)
+        results = [turn([P, 4, 512], F32, "wraw", 6, f"result{h}") for h in range(2)]
+        got_last, woven1 = {}, {}
 
-        def fetch1(i):
+        def fetch1(i, u):
             c0, width = CHUNKS[i]
-            got = turn([P, 2, 256], F32, "last", 2, f"got_last{i}")
-            for u in range(2):
-                nc.vector.tensor_copy(got[:, u, :width], page_t[1, 2 + u][:].indirect(lists["offs5"][:, c0 // 16 : (c0 + width) // 16]))
-            engine = nc.vector if i == len(CHUNKS) - 1 else nc.gpsimd
-            engine.tensor_tensor(
-                woven1_rows[:, c0 : c0 + width, 2:4], got[:, :, :width].rearrange("p u c -> p c u"),
-                gain_t[:, 1:2, 2:4].to_broadcast([P, width, 2]), MULT,
+            if u == 0:
+                got_last[i] = turn([P, 2, 256], F32, "last", 2, f"got_last{i}")
+            got = got_last[i][:, u, :width]
+            nc.vector.tensor_copy(got, page_t[1, 2 + u][:].indirect(lists["offs5"][:, c0 // 16 : (c0 + width) // 16]))
+            nc.scalar.activation(x1_rows[:, 2 + u, c0 : c0 + width], got, ACT.Copy, scale=gain_t[:, 1, 2 + u : 3 + u])
+
+        def weave1(i):
+            c0, width = CHUNKS[i]
+            woven1[i] = turn([P, PACK * 256], BF16, "woven1", 2, f"woven1{i}")[:, : PACK * width]
+            nc.vector.tensor_copy(
+                woven1[i].rearrange("p (c i t) -> p c t i", i=4, t=PACK),
+                x1_rows[:, :, c0 : c0 + width].rearrange("p t (c i) -> p c t i", i=4),
             )
 
-        results = [turn([P, 4, 512], F32, "wraw", 6, f"result{h}") for h in range(2)]
-
-        def finish(i):
+        def multiply1(i):
             c0, width = CHUNKS[i]
             x_codes = turn([P, 256], U32, "x1_codes", 2, f"x1_codes{i}")
             x_plane = turn([P, 256], U8, "x1_plane", 2, f"x1_plane{i}")
-            nc.vector.quantize_mx(out=x_codes[:, :width].bitcast(FP8X4), scales=x_plane[:, :width], in_=woven1[:, PACK * c0 : PACK * (c0 + width)])
+            nc.vector.quantize_mx(out=x_codes[:, :width].bitcast(FP8X4), scales=x_plane[:, :width], in_=woven1[i])
             last_pass(1, sums[i], x_codes[:, :width], x_plane[:, :width])
+
+        def finish(i):
+            c0, width = CHUNKS[i]
             result = results[c0 // 512][:, :, c0 % 512 : c0 % 512 + width]
             for n, spot in enumerate(sums[i]):
                 nc.scalar.activation(result[:, n, :], spot[0], ACT.Abs, bias=bias_t[:, n : n + 1])
             nc.sync.dma_start(out_rows[:, :, c0 : c0 + width], result)
 
-        for i in range(len(CHUNKS)):
-            fetch1(i)
-            if i > 0:
-                finish(i - 1)
-        finish(len(CHUNKS) - 1)
+        count = len(CHUNKS)
+        for i in range(count + 2):
+            if i < count:
+                fetch1(i, 0)
+            if 1 <= i <= count:
+                weave1(i - 1)
+            if i < count:
+                fetch1(i, 1)
+            if 1 <= i <= count:
+                multiply1(i - 1)
+            if i >= 2:
+                finish(i - 2)

@@ -129,22 +129,21 @@ def tile_list_glitch_catalogue_read_kernel(
         load_coup(0, 1, 1)
         load_wg("wg2", wg2, 1, 2)
         load_page(0, 1)
-        load_wg("wg1", wg1, 0, 1)
+        load_wg("wg1", wg1, 0, 2)
         load_list("offs3", offs3)
         load_list("offs5", offs5)
-        load_wg("wg1", wg1, 1, 2)
-        load_coup(0, 2, 2)
-        load_wg("wg2", wg2, 2, 4)
-        load_wg("wg1", wg1, 2, 4)
         raws["w3", 0, 1] = load_weight("w3_01", w3, 0, 1)
+        load_wg("wg1", wg1, 2, 4)
+        load_coup(0, 2, 2)
         load_page(0, 2)
+        load_page(0, 3)
         raws["w1", 0, 1] = load_weight("w1_01", w1, 0, 1)
         raws["w1", 1, 1] = load_weight("w1_11", w1, 1, 1)
+        load_wg("wg2", wg2, 2, 4)
         gain_t = load_rowvec("gain_t", gain)
-        load_coup(1, 0, 2)
-        load_page(0, 3)
         load_page(1, 0)
         load_page(1, 1)
+        load_coup(1, 0, 2)
         w4_w = [load_words(f"w4_w{a}", w4_words[a]) for a in range(2)]
         load_scales(w4_plane, w4_scales)
         bias_t = keep([P, 4], F32, "bias_t")
@@ -246,10 +245,10 @@ def tile_list_glitch_catalogue_read_kernel(
             nc.vector.tensor_tensor(h2, bank_b[:], h2, ADD)
             nc.vector.tensor_tensor(window(0, t, "offs4"), h2, wg_t["wg2", t], MULT)
 
-        def first1():
-            h1 = values("h1", 0, 0)
-            cosine(0, 0, h1)
-            return lambda: nc.vector.tensor_tensor(window(0, 0, "offs3"), h1, wg_t["wg1", 0], MULT)
+        def first1(t):
+            h1 = values("h1", 0, t)
+            cosine(0, t, h1)
+            return lambda: nc.vector.tensor_tensor(window(0, t, "offs3"), h1, wg_t["wg1", t], MULT)
 
         def stream2(b, t):
             h2 = values("h2", b, t)
@@ -259,7 +258,8 @@ def tile_list_glitch_catalogue_read_kernel(
             nc.scalar.copy(plain[:], bank_b[:])
             nc.gpsimd.tensor_tensor(h2, h2, coup_t[b, t], MULT)
             nc.gpsimd.tensor_tensor(h2, h2, plain[:], ADD)
-            nc.gpsimd.tensor_tensor(h2, h2, wg_t["wg2", t], MULT)
+            if t % 2 == 1:
+                nc.gpsimd.tensor_tensor(pairs["h2"][:], pairs["h2"][:], wg_pair["wg2", t - 1][:], MULT)
             return lambda: nc.vector.tensor_copy(window(b, t, "offs4"), h2)
 
         def stream1(b, t):
@@ -271,7 +271,7 @@ def tile_list_glitch_catalogue_read_kernel(
         first2(0)
         v_w = [gather_words(f"v_w{a}", tab_w[a], "offs") for a in range(2)]
         v_plane = gather_plane("v_plane", tab_plane, "offs")
-        quantise_weight(("w1", 0, 0), 0)
+        quantise_weight(("w1", 0, 0), 64)
         quantise_weight(("w1", 1, 0), 64)
         amp_m2 = keep([P, 2, PACK], F32, "amp_m2")
         nc.vector.tensor_scalar(amp_m2[:], amp_t[:], -2.0, None, MULT)
@@ -295,39 +295,46 @@ def tile_list_glitch_catalogue_read_kernel(
             )
             nc.vector.quantize_mx(out=x0_codes[:, cols].bitcast(FP8X4), scales=x0_plane[:, cols], in_=woven[:])
 
-        x1_rows = turn([P, PACK, NP], BF16, "wraw", 6, "x1_rows")
+        x1_pairs = turn([P, 2, NP, 2], BF16, "wraw", 6, "x1_pairs")
 
         def fetch1_whole(t):
             got = turn([P, NP], F32, "got", 3, f"got1{t}")
             nc.vector.tensor_copy(got[:], window(1, t, "offs5"))
-            nc.scalar.activation(x1_rows[:, t, :], got[:], ACT.Copy, scale=gain_t[:, 1, t : t + 1])
+            nc.scalar.activation(x1_pairs[:, 0, :, t], got[:], ACT.Copy, scale=gain_t[:, 1, t : t + 1])
 
-        put1, put2 = {(0, 0): first1(), (0, 1): stream1(0, 1)}, {}
+        put1, put2 = {(0, t): first1(t) for t in range(2)}, {}
         first2(1)
         put1[0, 0]()
-        fetch0(0)
         put1[0, 1]()
         for t in (2, 3):
-            put2[0, t], put1[0, t] = stream2(0, t), stream1(0, t)
+            put1[0, t] = stream1(0, t)
+        for t in (2, 3):
+            put2[0, t] = stream2(0, t)
+        fetch0(0)
         fetch0(1)
         quantise_weight(("w3", 0, 1), 0)
-        put2[0, 2]()
         put1[0, 2]()
-        fetch0(2)
+        put1[0, 3]()
         quantise_weight(("w1", 0, 1), 0)
         quantise_weight(("w1", 1, 1), 0)
+        put2[0, 2]()
         put2[0, 3]()
-        put1[0, 3]()
-        for t in range(PACK):
-            put2[1, t], put1[1, t] = stream2(1, t), stream1(1, t)
+        for t0 in (0, 2):
+            for t in (t0, t0 + 1):
+                put1[1, t] = stream1(1, t)
+            for t in (t0, t0 + 1):
+                put2[1, t] = stream2(1, t)
+        fetch0(2)
         fetch0(3)
+        put1[1, 0]()
+        put1[1, 1]()
+        put2[1, 0]()
+        put2[1, 1]()
         for t in range(2):
-            put2[1, t]()
-            put1[1, t]()
             quantise_x0(t)
             fetch1_whole(t)
-        put2[1, 2]()
-        put2[1, 3]()
+        put1[1, 2]()
+        put1[1, 3]()
 
         free_banks = list(banks)
 
@@ -352,8 +359,8 @@ def tile_list_glitch_catalogue_read_kernel(
         for c0, width in CHUNKS:
             sums.append(places(width))
             last_pass(0, sums[-1], x0_codes[:, c0 : c0 + width], x0_plane[:, c0 : c0 + width])
-        put1[1, 2]()
-        put1[1, 3]()
+        put2[1, 2]()
+        put2[1, 3]()
 
         out_rows = out.rearrange("(n p) j -> p n j", p=P)
         results = [turn([P, 4, 512], F32, "wraw", 6, f"result{h}") for h in range(2)]
@@ -365,14 +372,14 @@ def tile_list_glitch_catalogue_read_kernel(
                 got_last[i] = turn([P, 2, 256], F32, "last", 2, f"got_last{i}")
             got = got_last[i][:, u, :width]
             nc.vector.tensor_copy(got, page_t[1, 2 + u][:].indirect(lists["offs5"][:, c0 // 16 : (c0 + width) // 16]))
-            nc.scalar.activation(x1_rows[:, 2 + u, c0 : c0 + width], got, ACT.Copy, scale=gain_t[:, 1, 2 + u : 3 + u])
+            nc.scalar.activation(x1_pairs[:, 1, c0 : c0 + width, u], got, ACT.Copy, scale=gain_t[:, 1, 2 + u : 3 + u])
 
         def weave1(i):
             c0, width = CHUNKS[i]
             woven1[i] = turn([P, PACK * 256], BF16, "woven1", 2, f"woven1{i}")[:, : PACK * width]
             nc.vector.tensor_copy(
-                woven1[i].rearrange("p (c i t) -> p c t i", i=4, t=PACK),
-                x1_rows[:, :, c0 : c0 + width].rearrange("p t (c i) -> p c t i", i=4),
+                woven1[i].bitcast(I32).rearrange("p (c i h) -> p c h i", i=4, h=2),
+                x1_pairs[:, :, c0 : c0 + width, :].rearrange("p h c e -> p h (c e)").bitcast(I32).rearrange("p h (c i) -> p c h i", i=4),
             )
 
         def multiply1(i):

@@ -1,6 +1,7 @@
 from contextlib import ExitStack
 
 import concourse.mybir as mybir
+from concourse.masks import make_identity
 
 F32 = mybir.dt.float32
 BF16 = mybir.dt.bfloat16
@@ -20,8 +21,26 @@ FLOPS = 2 * K * H * S + 2 * 2 * K2 * H * S + 2 * H * N * NP
 P = 128
 PACK = 4
 KP = P * PACK
+BANK = 512
+QUAD = 32
+N_TILES = N // P
+LIST_COL = 16
+LINE = 4
 QUADRANTS = (0, 2, 1, 3)
 CHUNKS = [(0, 256), (256, 256), (512, 256), (768, 128), (896, 128)]
+CHUNK_MAX = 256
+LAST_PAIR = (1, 2)
+
+TABLE_BUFS = 3
+RAW_BUFS = 6
+ROUNDED_BUFS = 3
+PAGE_BUFS = 4
+COUP_BUFS = 1
+GOT_BUFS = 3
+STREAM_BUFS = 3
+LAST_BUFS = 2
+PLAIN_BUFS = 2
+CHUNK_BUFS = 2
 
 
 def tile_list_glitch_catalogue_read_kernel(
@@ -37,18 +56,18 @@ def tile_list_glitch_catalogue_read_kernel(
         def keep(shape, dtype, name):
             return held.tile(shape, dtype, name=name, align_bytes=64)
 
-        def turn(shape, dtype, tag, bufs, name):
+        def rotating(shape, dtype, tag, bufs, name):
             return ring.tile(shape, dtype, tag=tag, bufs=bufs, name=name, align_bytes=64)
 
-        banks = [psum.tile([P, 512], F32, name=f"bank{i}") for i in range(8)]
+        banks = [psum.tile([P, BANK], F32, name=f"bank{number}") for number in range(8)]
 
-        lists = {}
+        lists, raw_weights, coup_pairs, coup_rows, pages, wg_pairs, wg_rows = {}, {}, {}, {}, {}, {}, {}
 
         def load_list(name, src):
             lists[name] = keep(list(src.shape), U16, name + "_t")
             nc.sync.dma_start(lists[name][:], src)
 
-        def scale_tile(name, width):
+        def zeroed_plane(name, width):
             plane = keep([P, width], U8, name)
             nc.vector.memset(plane[:].bitcast(I32), 0)
             return plane
@@ -56,133 +75,123 @@ def tile_list_glitch_catalogue_read_kernel(
         def load_scales(plane, src):
             rows = PACK * src.shape[0]
             for q in QUADRANTS:
-                nc.sync.dma_start(plane[32 * q : 32 * q + rows, :].bitcast(I32), src[:, 4 * q : 4 * q + 4, :].bitcast(I32))
+                nc.sync.dma_start(
+                    plane[QUAD * q : QUAD * q + rows, :].bitcast(I32), src[:, 4 * q : 4 * q + 4, :].bitcast(I32)
+                )
 
-        def load_words(name, src):
-            words = turn([P, src.shape[1]], I32, "table", 3, name) if src.shape[1] == T else keep([P, src.shape[1]], I32, name)
-            nc.sync.dma_start(words[:], src.rearrange("p n i -> p (n i)").bitcast(I32))
+        def load_words(words, src):
+            nc.sync.dma_start(words[:], src.rearrange("p c j -> p (c j)").bitcast(I32))
             return words
 
+        def load_table(name, src):
+            return load_words(rotating([P, T], I32, "table", TABLE_BUFS, name), src)
+
         def load_weight(name, w, a, b):
-            raw = turn([P, PACK, KP], F32, "wraw", 6, name)
-            nc.sync.dma_start(raw[:], w[KP * a : KP * (a + 1), KP * b : KP * (b + 1)].rearrange("(p j) c -> p j c", j=PACK))
-            return raw
+            raw = rotating([P, PACK, KP], F32, "wraw", RAW_BUFS, f"{name}_{a}{b}")
+            block = w[KP * a : KP * (a + 1), KP * b : KP * (b + 1)]
+            nc.sync.dma_start(raw[:], block.rearrange("(p j) c -> p j c", j=PACK))
+            raw_weights[name, a, b] = raw
 
-        def rows_of(x, b, t):
-            return x[KP * b : KP * (b + 1), :].rearrange("(p t) c -> p t c", t=PACK)[:, t, :]
-
-        coup_t, page_t, coup_pair = {}, {}, {}
+        def by_slice(x, b):
+            return x[KP * b : KP * (b + 1), :].rearrange("(p t) c -> p t c", t=PACK)
 
         def load_coup(b, t0, count):
-            rows = turn([P, 2, S], F32, "coup", 2, f"coup{b}{t0}") if t0 % 2 == 0 else coup_pair[0]
-            coup_pair[0] = rows
-            src = coup[KP * b : KP * (b + 1), :].rearrange("(p t) c -> p t c", t=PACK)
-            nc.sync.dma_start(rows[:, t0 % 2 : t0 % 2 + count, :], src[:, t0 : t0 + count, :])
+            if t0 % 2 == 0:
+                coup_pairs[b, t0] = rotating([P, 2, S], F32, "coup", COUP_BUFS, f"coup{b}{t0}")
+            pair = coup_pairs[b, t0 - t0 % 2]
+            nc.sync.dma_start(pair[:, t0 % 2 : t0 % 2 + count, :], by_slice(coup, b)[:, t0 : t0 + count, :])
             for t in range(t0, t0 + count):
-                coup_t[b, t] = rows[:, t % 2, :]
+                coup_rows[b, t] = pair[:, t % 2, :]
 
         def load_page(b, t):
-            page_t[b, t] = turn([P, T2], F32, "page", 4, f"page{b}{t}")
-            nc.sync.dma_start(page_t[b, t][:], rows_of(page0, b, t))
+            pages[b, t] = rotating([P, T2], F32, "page", PAGE_BUFS, f"page{b}{t}")
+            nc.sync.dma_start(pages[b, t][:], by_slice(page0, b)[:, t, :])
 
-        wg_t = {}
+        def load_wg(name, src):
+            for t0 in (0, 2):
+                wg_pairs[name, t0] = keep([P, 2, S], F32, f"{name}_{t0}")
+            for t in range(PACK):
+                wg_rows[name, t] = wg_pairs[name, t - t % 2][:, t % 2, :]
+            nc.sync.dma_start(wg_rows[name, PACK - 1], src)
 
-        wg_pair = {}
+        def load_row_factors(name, src):
+            factors = keep([P, 2, PACK], F32, name)
+            nc.sync.dma_start(factors[:], src.rearrange("(b p t) -> p b t", b=2, t=PACK))
+            return factors
 
-        def load_wg(name, src, t0, t1):
-            if t0 % 2 == 0:
-                wg_pair[name, t0] = keep([P, 2, S], F32, f"{name}_{t0}")
-            dealt = wg_pair[name, t0 - t0 % 2]
-            for q in QUADRANTS:
-                nc.sync.dma_start(dealt[32 * q : 32 * (q + 1), t0 % 2 : t0 % 2 + t1 - t0, :], src.rearrange("(p t) c -> p t c", t=PACK)[:, t0:t1, :])
-            for t in range(t0, t1):
-                wg_t[name, t] = dealt[:, t % 2, :]
+        tab2_plane = zeroed_plane("tab2_plane", T)
+        w2_plane_raw = zeroed_plane("w2_plane_raw", H)
+        tab_plane = zeroed_plane("tab_plane", T)
+        w4_plane = zeroed_plane("w4_plane", N)
 
-        def load_rowvec(name, src):
-            vec = keep([P, 2, PACK], F32, name)
-            nc.sync.dma_start(vec[:], src.rearrange("(b p t) -> p b t", b=2, t=PACK))
-            return vec
-
-        tab2_plane = scale_tile("tab2_plane", T)
-        w2_plane_raw = scale_tile("w2_plane_raw", H)
-        tab_plane = scale_tile("tab_plane", T)
-        w4_plane = scale_tile("w4_plane", N)
-
-        raws = {}
         load_list("offs2", offs2)
-        tab2_w = load_words("tab2_w", tab2_words[0])
+        tab2_w = load_table("tab2_w", tab2_words[0])
         load_scales(tab2_plane, tab2_scales)
-        raws["w3", 0, 0] = load_weight("w3_00", w3, 0, 0)
+        load_wg("wg2", wg2)
+        load_weight("w3", w3, 0, 0)
         w2_raw = keep([P, 2 * H], U8, "w2_raw")
         nc.sync.dma_start(w2_raw[:].bitcast(I32), w2_words[0].bitcast(I32))
         load_scales(w2_plane_raw, w2_scales)
         load_coup(0, 0, 1)
         load_page(0, 0)
-        load_wg("wg2", wg2, 0, 1)
         load_list("offs4", offs4)
+        load_wg("wg1", wg1)
         load_list("offs", offs)
-        tab_w = [load_words(f"tab_w{a}", tab_words[a]) for a in range(2)]
+        tab_w = [load_table(f"tab_w{a}", tab_words[a]) for a in range(2)]
         load_scales(tab_plane, tab_scales)
-        raws["w1", 0, 0] = load_weight("w1_00", w1, 0, 0)
-        raws["w1", 1, 0] = load_weight("w1_10", w1, 1, 0)
-        amp_t = load_rowvec("amp_t", amp)
+        load_weight("w1", w1, 0, 0)
+        load_weight("w1", w1, 1, 0)
+        amp_t = load_row_factors("amp_t", amp)
         load_coup(0, 1, 1)
-        load_wg("wg2", wg2, 1, 2)
         load_page(0, 1)
-        load_wg("wg1", wg1, 0, 2)
         load_list("offs3", offs3)
+        load_weight("w3", w3, 0, 1)
         load_list("offs5", offs5)
-        raws["w3", 0, 1] = load_weight("w3_01", w3, 0, 1)
-        load_wg("wg1", wg1, 2, 4)
-        load_coup(0, 2, 2)
         load_page(0, 2)
         load_page(0, 3)
-        raws["w1", 0, 1] = load_weight("w1_01", w1, 0, 1)
-        raws["w1", 1, 1] = load_weight("w1_11", w1, 1, 1)
-        load_wg("wg2", wg2, 2, 4)
-        gain_t = load_rowvec("gain_t", gain)
+        load_weight("w1", w1, 0, 1)
+        load_weight("w1", w1, 1, 1)
+        load_coup(0, 2, 2)
+        gain_t = load_row_factors("gain_t", gain)
         load_page(1, 0)
         load_page(1, 1)
         load_coup(1, 0, 2)
-        w4_w = [load_words(f"w4_w{a}", w4_words[a]) for a in range(2)]
+        w4_w = [load_words(keep([P, N], I32, f"w4_w{a}"), w4_words[a]) for a in range(2)]
         load_scales(w4_plane, w4_scales)
-        bias_t = keep([P, 4], F32, "bias_t")
+        bias_t = keep([P, N_TILES], F32, "bias_t")
         with nc.allow_non_contiguous_dma(reason="one bias value for each output row"):
             nc.sync.dma_start(bias_t[:], bias.rearrange("(n p) -> p n", p=P))
         load_page(1, 2)
         load_page(1, 3)
         load_coup(1, 2, 2)
 
-        def gather_words(name, words, lst):
+        def gather_words(name, words, list_name):
             picked = keep([P, S], U32, name)
-            nc.vector.tensor_copy(picked[:], words[:].bitcast(U32).indirect(lists[lst][:]))
+            nc.vector.tensor_copy(picked[:], words[:].bitcast(U32).indirect(lists[list_name][:]))
             return picked
 
-        def gather_plane(name, plane, lst):
+        def gather_plane(name, plane, list_name):
             picked = keep([P, S], U8, name)
-            nc.vector.tensor_copy(picked[:], plane[:].indirect(lists[lst][:]))
+            nc.vector.tensor_copy(picked[:], plane[:].indirect(lists[list_name][:]))
             return picked
 
         codes, planes = {}, {}
 
-        def quantise_weight(key, split):
-            raw = raws[key]
-            name = "%s_%d%d" % key
-            rounded = turn([P, PACK * KP], BF16, "wbf", 3, name + "_bf")
+        def quantise_weight(name, a, b, on_scalar):
+            rounded = rotating([P, PACK * KP], BF16, "wbf", ROUNDED_BUFS, f"{name}_{a}{b}_bf")
             dst = rounded[:].rearrange("p (t m j) -> p m j t", t=PACK, j=PACK)
-            src = raw[:].rearrange("p j (m t) -> p m j t", t=PACK)
-            if split:
-                nc.scalar.copy(dst[:, :split], src[:, :split])
-                nc.vector.tensor_copy(dst[:, split:], src[:, split:])
-            else:
-                nc.scalar.copy(dst, src)
-            codes[key] = keep([P, KP], U32, name + "_codes")
-            planes[key] = keep([P, KP], U8, name + "_plane")
-            nc.vector.quantize_mx(out=codes[key][:].bitcast(FP8X4), scales=planes[key][:], in_=rounded[:])
+            src = raw_weights[name, a, b][:].rearrange("p j (m t) -> p m j t", t=PACK)
+            if on_scalar > 0:
+                nc.scalar.copy(dst[:, :on_scalar], src[:, :on_scalar])
+            if on_scalar < P:
+                nc.vector.tensor_copy(dst[:, on_scalar:], src[:, on_scalar:])
+            codes[name, a, b] = keep([P, KP], U32, f"{name}_{a}{b}_codes")
+            planes[name, a, b] = keep([P, KP], U8, f"{name}_{a}{b}_plane")
+            nc.vector.quantize_mx(out=codes[name, a, b][:].bitcast(FP8X4), scales=planes[name, a, b][:], in_=rounded[:])
 
         v2_w = gather_words("v2_w", tab2_w, "offs2")
         v2_plane = gather_plane("v2_plane", tab2_plane, "offs2")
-        quantise_weight(("w3", 0, 0), 64)
+        quantise_weight("w3", 0, 0, on_scalar=0)
 
         w2_dealt = keep([P, 2 * H], U8, "w2_dealt")
         w2_plane = keep([P, H], U8, "w2_plane")
@@ -196,24 +205,42 @@ def tile_list_glitch_catalogue_read_kernel(
                 w2_plane_raw[:, KP * b : KP * (b + 1)].rearrange("p (m t) -> p m t", t=PACK),
             )
 
-        used = []
+        taken = []
 
         def next_bank():
-            used.append(None)
-            return banks[4 + (len(used) - 1) % 4]
+            taken.append(banks[4 + len(taken) % 4])
+            return taken[-1]
 
-        def products2(b, t, bank_a, bank_b):
+        identity = keep([P, P], F32, "identity")
+        make_identity(nc, identity[:])
+
+        def transpose_blocks(bank, src):
+            for c in range(BANK // P):
+                nc.tensor.transpose(bank[:, P * c : P * (c + 1)], src[:, P * c : P * (c + 1)], identity[:])
+
+        def deal_wg(name):
+            turned = next_bank()
+            transpose_blocks(turned, wg_rows[name, PACK - 1])
+            rows_of_slice = turned[:].rearrange("p (c s t) -> p c t s", c=S // P, t=PACK)
+            shape = [P, S // P, P // QUAD, QUAD]
+            for t in range(PACK):
+                spread = rotating(shape, F32, "got", GOT_BUFS, f"{name}_spread{t}")
+                nc.scalar.copy(spread[:], rows_of_slice[:, :, t : t + 1, :].to_broadcast(shape))
+                dealt = next_bank()
+                transpose_blocks(dealt, spread[:].rearrange("p c q s -> p (c q s)"))
+                nc.scalar.copy(wg_rows[name, t], dealt[:])
+
+        def products2(b, t, with_w2, with_w3):
             cols = slice(P * t, P * (t + 1))
             c0 = KP * b + P * t
             nc.tensor.matmul_mx(
-                out=bank_a[:], lhsT=w2_dealt[:, 2 * c0 : 2 * (c0 + P)].bitcast(FP4X4), lhsT_scale=w2_plane[:, c0 : c0 + P],
+                out=with_w2[:], lhsT=w2_dealt[:, 2 * c0 : 2 * (c0 + P)].bitcast(FP4X4), lhsT_scale=w2_plane[:, c0 : c0 + P],
                 rhs=v2_w[:].bitcast(FP8X4), rhs_scale=v2_plane[:], start=True, stop=True,
             )
             nc.tensor.matmul_mx(
-                out=bank_b[:], lhsT=codes["w3", 0, b][:, cols].bitcast(FP8X4), lhsT_scale=planes["w3", 0, b][:, cols],
+                out=with_w3[:], lhsT=codes["w3", 0, b][:, cols].bitcast(FP8X4), lhsT_scale=planes["w3", 0, b][:, cols],
                 rhs=v2_w[:].bitcast(FP8X4), rhs_scale=v2_plane[:], start=True, stop=True,
             )
-            return bank_a, bank_b
 
         def cosine(b, t, h1):
             cols = slice(P * t, P * (t + 1))
@@ -227,127 +254,126 @@ def tile_list_glitch_catalogue_read_kernel(
             nc.scalar.activation(h1, h1, ACT.Square)
             nc.scalar.activation(h1, h1, ACT.Identity, bias=amp_t[:, b, t : t + 1], scale=amp_m2[:, b, t : t + 1])
 
-        def window(b, t, lst):
-            return page_t[b, t][:].indirect(lists[lst][:])
+        def window(b, t, list_name):
+            return pages[b, t][:].indirect(lists[list_name][:])
 
-        pairs = {}
+        stream_pairs = {}
 
-        def values(stream, b, t):
+        def stream_values(stream, b, t):
             if t % 2 == 0:
-                tag, bufs = ("last", 2) if (b, t) == (1, 2) else (stream, 3)
-                pairs[stream] = turn([P, 2, S], F32, tag, bufs, f"{stream}_{b}{t}")
-            return pairs[stream][:, t % 2, :]
+                tag, bufs = ("last", LAST_BUFS) if (b, t) == LAST_PAIR else (stream, STREAM_BUFS)
+                stream_pairs[stream] = rotating([P, 2, S], F32, tag, bufs, f"{stream}_{b}{t}")
+            return stream_pairs[stream][:, t % 2, :]
 
-        def first2(t):
-            h2 = values("h2", 0, t)
-            bank_a, bank_b = products2(0, t, banks[2 * t], banks[2 * t + 1])
-            nc.vector.tensor_tensor(h2, bank_a[:], coup_t[0, t], MULT)
-            nc.vector.tensor_tensor(h2, bank_b[:], h2, ADD)
-            nc.vector.tensor_tensor(window(0, t, "offs4"), h2, wg_t["wg2", t], MULT)
+        def first_pair_stream2(t):
+            h2 = stream_values("h2", 0, t)
+            with_w2, with_w3 = banks[2 * t], banks[2 * t + 1]
+            products2(0, t, with_w2, with_w3)
+            nc.vector.tensor_tensor(h2, with_w2[:], coup_rows[0, t], MULT)
+            nc.vector.tensor_tensor(h2, with_w3[:], h2, ADD)
+            nc.vector.tensor_tensor(window(0, t, "offs4"), h2, wg_rows["wg2", t], MULT)
 
-        def first1(t):
-            h1 = values("h1", 0, t)
+        def first_pair_stream1(t):
+            h1 = stream_values("h1", 0, t)
             cosine(0, t, h1)
-            return lambda: nc.vector.tensor_tensor(window(0, t, "offs3"), h1, wg_t["wg1", t], MULT)
-
-        def stream2(b, t):
-            h2 = values("h2", b, t)
-            plain = turn([P, S], F32, "plain", 2, f"plain_{b}{t}")
-            bank_a, bank_b = products2(b, t, next_bank(), next_bank())
-            nc.scalar.copy(h2, bank_a[:])
-            nc.scalar.copy(plain[:], bank_b[:])
-            nc.gpsimd.tensor_tensor(h2, h2, coup_t[b, t], MULT)
-            nc.gpsimd.tensor_tensor(h2, h2, plain[:], ADD)
-            if t % 2 == 1:
-                nc.gpsimd.tensor_tensor(pairs["h2"][:], pairs["h2"][:], wg_pair["wg2", t - 1][:], MULT)
-            return lambda: nc.vector.tensor_copy(window(b, t, "offs4"), h2)
+            return lambda: nc.vector.tensor_tensor(window(0, t, "offs3"), h1, wg_rows["wg1", t], MULT)
 
         def stream1(b, t):
-            h1 = values("h1", b, t)
+            h1 = stream_values("h1", b, t)
             cosine(b, t, h1)
-            nc.gpsimd.tensor_tensor(h1, h1, wg_t["wg1", t], MULT)
+            nc.gpsimd.tensor_tensor(h1, h1, wg_rows["wg1", t], MULT)
             return lambda: nc.vector.tensor_copy(window(b, t, "offs3"), h1)
 
-        first2(0)
+        def stream2(b, t):
+            h2 = stream_values("h2", b, t)
+            plain = rotating([P, S], F32, "plain", PLAIN_BUFS, f"plain_{b}{t}")
+            with_w2, with_w3 = next_bank(), next_bank()
+            products2(b, t, with_w2, with_w3)
+            nc.scalar.copy(h2, with_w2[:])
+            nc.scalar.copy(plain[:], with_w3[:])
+            nc.gpsimd.tensor_tensor(h2, h2, coup_rows[b, t], MULT)
+            nc.gpsimd.tensor_tensor(h2, h2, plain[:], ADD)
+            if t % 2 == 1:
+                nc.gpsimd.tensor_tensor(stream_pairs["h2"][:], stream_pairs["h2"][:], wg_pairs["wg2", t - 1][:], MULT)
+            return lambda: nc.vector.tensor_copy(window(b, t, "offs4"), h2)
+
+        def both_streams(b, t0):
+            puts1 = [stream1(b, t) for t in (t0, t0 + 1)]
+            puts2 = [stream2(b, t) for t in (t0, t0 + 1)]
+            return puts1, puts2
+
+        def scatter(puts):
+            for put in puts:
+                put()
+
+        deal_wg("wg2")
+        first_pair_stream2(0)
+        deal_wg("wg1")
         v_w = [gather_words(f"v_w{a}", tab_w[a], "offs") for a in range(2)]
         v_plane = gather_plane("v_plane", tab_plane, "offs")
-        quantise_weight(("w1", 0, 0), 64)
-        quantise_weight(("w1", 1, 0), 64)
+        for a in range(2):
+            quantise_weight("w1", a, 0, on_scalar=P // 2)
         amp_m2 = keep([P, 2, PACK], F32, "amp_m2")
         nc.vector.tensor_scalar(amp_m2[:], amp_t[:], -2.0, None, MULT)
 
-        x0_rows = turn([P, PACK, NP], BF16, "table", 3, "x0_rows")
-
-        def fetch0(t):
-            got = turn([P, NP], F32, "got", 3, f"got0{t}")
-            nc.vector.tensor_copy(got[:], page_t[0, t][:].indirect(lists["offs5"][:]))
-            nc.scalar.activation(x0_rows[:, t, :], got[:], ACT.Copy, scale=gain_t[:, 0, t : t + 1])
-
+        x0_rows = rotating([P, PACK, NP], BF16, "table", TABLE_BUFS, "x0_rows")
         x0_codes = keep([P, NP], U32, "x0_codes")
         x0_plane = keep([P, NP], U8, "x0_plane")
+        x1_pairs = rotating([P, 2, NP, 2], BF16, "wraw", RAW_BUFS, "x1_pairs")
+        halves = [slice(0, NP // 2), slice(NP // 2, NP)]
 
-        def quantise_x0(h):
-            cols = slice(512 * h, 512 * (h + 1))
-            woven = turn([P, PACK * 512], BF16, "table", 3, f"woven0{h}")
+        def fetch(b, t, rounded):
+            got = rotating([P, NP], F32, "got", GOT_BUFS, f"got{b}{t}")
+            nc.vector.tensor_copy(got[:], window(b, t, "offs5"))
+            nc.scalar.activation(rounded, got[:], ACT.Copy, scale=gain_t[:, b, t : t + 1])
+
+        def interleave_x0(h):
+            woven = rotating([P, PACK * NP // 2], BF16, "table", TABLE_BUFS, f"woven0{h}")
             nc.scalar.copy(
-                woven[:].rearrange("p (c i t) -> p c t i", i=4, t=PACK),
-                x0_rows[:, :, cols].rearrange("p t (c i) -> p c t i", i=4),
+                woven[:].rearrange("p (c l t) -> p c t l", l=LINE, t=PACK),
+                x0_rows[:, :, halves[h]].rearrange("p t (c l) -> p c t l", l=LINE),
             )
-            nc.vector.quantize_mx(out=x0_codes[:, cols].bitcast(FP8X4), scales=x0_plane[:, cols], in_=woven[:])
+            return woven
 
-        x1_pairs = turn([P, 2, NP, 2], BF16, "wraw", 6, "x1_pairs")
+        puts1 = [first_pair_stream1(t) for t in range(2)]
+        first_pair_stream2(1)
+        scatter(puts1)
 
-        def fetch1_whole(t):
-            got = turn([P, NP], F32, "got", 3, f"got1{t}")
-            nc.vector.tensor_copy(got[:], window(1, t, "offs5"))
-            nc.scalar.activation(x1_pairs[:, 0, :, t], got[:], ACT.Copy, scale=gain_t[:, 1, t : t + 1])
+        puts1, puts2 = both_streams(0, 2)
+        for t in (0, 1):
+            fetch(0, t, x0_rows[:, t, :])
+        quantise_weight("w3", 0, 1, on_scalar=P)
+        scatter(puts1)
+        for a in range(2):
+            quantise_weight("w1", a, 1, on_scalar=P)
+        scatter(puts2)
 
-        put1, put2 = {(0, t): first1(t) for t in range(2)}, {}
-        first2(1)
-        put1[0, 0]()
-        put1[0, 1]()
+        puts1, puts2 = both_streams(1, 0)
         for t in (2, 3):
-            put1[0, t] = stream1(0, t)
-        for t in (2, 3):
-            put2[0, t] = stream2(0, t)
-        fetch0(0)
-        fetch0(1)
-        quantise_weight(("w3", 0, 1), 0)
-        put1[0, 2]()
-        put1[0, 3]()
-        quantise_weight(("w1", 0, 1), 0)
-        quantise_weight(("w1", 1, 1), 0)
-        put2[0, 2]()
-        put2[0, 3]()
-        for t0 in (0, 2):
-            for t in (t0, t0 + 1):
-                put1[1, t] = stream1(1, t)
-            for t in (t0, t0 + 1):
-                put2[1, t] = stream2(1, t)
-        fetch0(2)
-        fetch0(3)
-        put1[1, 0]()
-        put1[1, 1]()
-        put2[1, 0]()
-        put2[1, 1]()
-        for t in range(2):
-            quantise_x0(t)
-            fetch1_whole(t)
-        put1[1, 2]()
-        put1[1, 3]()
+            fetch(0, t, x0_rows[:, t, :])
+        woven0 = [interleave_x0(h) for h in range(2)]
+        last_puts1, last_puts2 = both_streams(*LAST_PAIR)
+        scatter(puts1)
+        scatter(puts2)
+
+        for h in range(2):
+            nc.vector.quantize_mx(out=x0_codes[:, halves[h]].bitcast(FP8X4), scales=x0_plane[:, halves[h]], in_=woven0[h][:])
+            fetch(1, h, x1_pairs[:, 0, :, h])
+        scatter(last_puts1)
 
         free_banks = list(banks)
 
         def places(width):
-            per_bank = 512 // width
+            per_bank = BANK // width
             spots = []
-            for n in range(4):
-                if n % per_bank == 0:
+            for n in range(N_TILES):
+                rank = n % per_bank
+                if rank == 0:
                     bank = free_banks.pop(0)
-                spots.append((bank[:, width * (n % per_bank) : width * (n % per_bank + 1)], n % per_bank == 0, n % per_bank == per_bank - 1))
+                spots.append((bank[:, width * rank : width * (rank + 1)], rank == 0, rank == per_bank - 1))
             return spots
 
-        def last_pass(a, spots, x_codes, x_plane):
+        def last_product_pass(a, spots, x_codes, x_plane):
             for n, (place, first, last) in enumerate(spots):
                 cols = slice(P * n, P * (n + 1))
                 nc.tensor.matmul_mx(
@@ -358,40 +384,42 @@ def tile_list_glitch_catalogue_read_kernel(
         sums = []
         for c0, width in CHUNKS:
             sums.append(places(width))
-            last_pass(0, sums[-1], x0_codes[:, c0 : c0 + width], x0_plane[:, c0 : c0 + width])
-        put2[1, 2]()
-        put2[1, 3]()
+            last_product_pass(0, sums[-1], x0_codes[:, c0 : c0 + width], x0_plane[:, c0 : c0 + width])
+        scatter(last_puts2)
 
-        out_rows = out.rearrange("(n p) j -> p n j", p=P)
-        results = [turn([P, 4, 512], F32, "wraw", 6, f"result{h}") for h in range(2)]
+        out_rows = out.rearrange("(n p) c -> p n c", p=P)
+        results = [rotating([P, N_TILES, NP // 2], F32, "wraw", RAW_BUFS, f"result{h}") for h in range(2)]
         got_last, woven1 = {}, {}
 
-        def fetch1(i, u):
+        def fetch_chunk(i, u):
             c0, width = CHUNKS[i]
             if u == 0:
-                got_last[i] = turn([P, 2, 256], F32, "last", 2, f"got_last{i}")
+                got_last[i] = rotating([P, 2, CHUNK_MAX], F32, "last", LAST_BUFS, f"got_last{i}")
             got = got_last[i][:, u, :width]
-            nc.vector.tensor_copy(got, page_t[1, 2 + u][:].indirect(lists["offs5"][:, c0 // 16 : (c0 + width) // 16]))
+            offsets = lists["offs5"][:, c0 // LIST_COL : (c0 + width) // LIST_COL]
+            nc.vector.tensor_copy(got, pages[1, 2 + u][:].indirect(offsets))
             nc.scalar.activation(x1_pairs[:, 1, c0 : c0 + width, u], got, ACT.Copy, scale=gain_t[:, 1, 2 + u : 3 + u])
 
-        def weave1(i):
+        def interleave_chunk(i):
             c0, width = CHUNKS[i]
-            woven1[i] = turn([P, PACK * 256], BF16, "woven1", 2, f"woven1{i}")[:, : PACK * width]
+            woven1[i] = rotating([P, PACK * CHUNK_MAX], BF16, "woven1", CHUNK_BUFS, f"woven1{i}")[:, : PACK * width]
+            words = x1_pairs[:, :, c0 : c0 + width, :].rearrange("p pair c u -> p pair (c u)").bitcast(I32)
             nc.vector.tensor_copy(
-                woven1[i].bitcast(I32).rearrange("p (c i h) -> p c h i", i=4, h=2),
-                x1_pairs[:, :, c0 : c0 + width, :].rearrange("p h c e -> p h (c e)").bitcast(I32).rearrange("p h (c i) -> p c h i", i=4),
+                woven1[i].bitcast(I32).rearrange("p (c l pair) -> p c pair l", l=LINE, pair=2),
+                words.rearrange("p pair (c l) -> p c pair l", l=LINE),
             )
 
-        def multiply1(i):
-            c0, width = CHUNKS[i]
-            x_codes = turn([P, 256], U32, "x1_codes", 2, f"x1_codes{i}")
-            x_plane = turn([P, 256], U8, "x1_plane", 2, f"x1_plane{i}")
+        def multiply_chunk(i):
+            width = CHUNKS[i][1]
+            x_codes = rotating([P, CHUNK_MAX], U32, "x1_codes", CHUNK_BUFS, f"x1_codes{i}")
+            x_plane = rotating([P, CHUNK_MAX], U8, "x1_plane", CHUNK_BUFS, f"x1_plane{i}")
             nc.vector.quantize_mx(out=x_codes[:, :width].bitcast(FP8X4), scales=x_plane[:, :width], in_=woven1[i])
-            last_pass(1, sums[i], x_codes[:, :width], x_plane[:, :width])
+            last_product_pass(1, sums[i], x_codes[:, :width], x_plane[:, :width])
 
-        def finish(i):
+        def store_chunk(i):
             c0, width = CHUNKS[i]
-            result = results[c0 // 512][:, :, c0 % 512 : c0 % 512 + width]
+            start = c0 % (NP // 2)
+            result = results[c0 // (NP // 2)][:, :, start : start + width]
             for n, spot in enumerate(sums[i]):
                 nc.scalar.activation(result[:, n, :], spot[0], ACT.Abs, bias=bias_t[:, n : n + 1])
             nc.sync.dma_start(out_rows[:, :, c0 : c0 + width], result)
@@ -399,12 +427,12 @@ def tile_list_glitch_catalogue_read_kernel(
         count = len(CHUNKS)
         for i in range(count + 2):
             if i < count:
-                fetch1(i, 0)
+                fetch_chunk(i, 0)
             if 1 <= i <= count:
-                weave1(i - 1)
+                interleave_chunk(i - 1)
             if i < count:
-                fetch1(i, 1)
+                fetch_chunk(i, 1)
             if 1 <= i <= count:
-                multiply1(i - 1)
+                multiply_chunk(i - 1)
             if i >= 2:
-                finish(i - 2)
+                store_chunk(i - 2)

from contextlib import ExitStack

import concourse.mybir as mybir
from concourse.masks import make_identity

F32 = mybir.dt.float32
BF16 = mybir.dt.bfloat16
I32 = mybir.dt.int32
U32 = mybir.dt.uint32
U16 = mybir.dt.uint16
U8 = mybir.dt.uint8
FP8X4 = mybir.dt.float8_e4m3fn_x4
FP4X4 = mybir.dt.float4_e2m1fn_x4
ACT = mybir.ActivationFunctionType
MULT = mybir.AluOpType.mult
ADD = mybir.AluOpType.add

K, K2, T, S, H, T2, NP, N = 1024, 512, 2048, 512, 1024, 2048, 1024, 512
FLOPS = 2 * K * H * S + 2 * 2 * K2 * H * S + 2 * H * N * NP

P = 128
PACK = 4
KP = P * PACK
BANK = 512
QUAD = 32
N_TILES = N // P
LIST_COL = 16
LINE = 4
QUADRANTS = (0, 2, 1, 3)
CHUNKS = [(0, 256), (256, 256), (512, 256), (768, 128), (896, 128)]
CHUNK_MAX = 256
LAST_PAIR = (1, 2)

TABLE_BUFS = 3
RAW_BUFS = 6
ROUNDED_BUFS = 3
PAGE_BUFS = 4
COUP_BUFS = 1
GOT_BUFS = 3
STREAM_BUFS = 3
LAST_BUFS = 2
PLAIN_BUFS = 2
CHUNK_BUFS = 2


def tile_list_glitch_catalogue_read_kernel(
    tc, tab_words, tab_scales, tab2_words, tab2_scales, offs, offs2, offs3, offs4, offs5,
    w1, amp, w2_words, w2_scales, coup, w3, page0, wg1, wg2, gain, w4_words, w4_scales, bias, out,
):
    nc = tc.nc
    with ExitStack() as ctx:
        held = ctx.enter_context(tc.tile_pool(name="held", bufs=1))
        ring = ctx.enter_context(tc.tile_pool(name="ring", bufs=2))
        psum = ctx.enter_context(tc.psum_pool(name="psum", bufs=1))

        def keep(shape, dtype, name):
            return held.tile(shape, dtype, name=name, align_bytes=64)

        def rotating(shape, dtype, tag, bufs, name):
            return ring.tile(shape, dtype, tag=tag, bufs=bufs, name=name, align_bytes=64)

        banks = [psum.tile([P, BANK], F32, name=f"bank{number}") for number in range(8)]

        lists, raw_weights, coup_pairs, coup_rows, pages, wg_pairs, wg_rows = {}, {}, {}, {}, {}, {}, {}

        def load_list(name, src):
            lists[name] = keep(list(src.shape), U16, name + "_t")
            nc.sync.dma_start(lists[name][:], src)

        def zeroed_plane(name, width):
            plane = keep([P, width], U8, name)
            nc.vector.memset(plane[:].bitcast(I32), 0)
            return plane

        def load_scales(plane, src):
            rows = PACK * src.shape[0]
            for q in QUADRANTS:
                nc.sync.dma_start(
                    plane[QUAD * q : QUAD * q + rows, :].bitcast(I32), src[:, 4 * q : 4 * q + 4, :].bitcast(I32)
                )

        def load_words(words, src):
            nc.sync.dma_start(words[:], src.rearrange("p c j -> p (c j)").bitcast(I32))
            return words

        def load_table(name, src):
            return load_words(rotating([P, T], I32, "table", TABLE_BUFS, name), src)

        def load_weight(name, w, a, b):
            raw = rotating([P, PACK, KP], F32, "wraw", RAW_BUFS, f"{name}_{a}{b}")
            block = w[KP * a : KP * (a + 1), KP * b : KP * (b + 1)]
            nc.sync.dma_start(raw[:], block.rearrange("(p j) c -> p j c", j=PACK))
            raw_weights[name, a, b] = raw

        def by_slice(x, b):
            return x[KP * b : KP * (b + 1), :].rearrange("(p t) c -> p t c", t=PACK)

        def load_coup(b, t0, count):
            if t0 % 2 == 0:
                coup_pairs[b, t0] = rotating([P, 2, S], F32, "coup", COUP_BUFS, f"coup{b}{t0}")
            pair = coup_pairs[b, t0 - t0 % 2]
            nc.sync.dma_start(pair[:, t0 % 2 : t0 % 2 + count, :], by_slice(coup, b)[:, t0 : t0 + count, :])
            for t in range(t0, t0 + count):
                coup_rows[b, t] = pair[:, t % 2, :]

        def load_page(b, t):
            pages[b, t] = rotating([P, T2], F32, "page", PAGE_BUFS, f"page{b}{t}")
            nc.sync.dma_start(pages[b, t][:], by_slice(page0, b)[:, t, :])

        def load_wg(name, src):
            for t0 in (0, 2):
                wg_pairs[name, t0] = keep([P, 2, S], F32, f"{name}_{t0}")
            for t in range(PACK):
                wg_rows[name, t] = wg_pairs[name, t - t % 2][:, t % 2, :]
            nc.sync.dma_start(wg_rows[name, PACK - 1], src)

        def load_row_factors(name, src):
            factors = keep([P, 2, PACK], F32, name)
            nc.sync.dma_start(factors[:], src.rearrange("(b p t) -> p b t", b=2, t=PACK))
            return factors

        tab2_plane = zeroed_plane("tab2_plane", T)
        w2_plane_raw = zeroed_plane("w2_plane_raw", H)
        tab_plane = zeroed_plane("tab_plane", T)
        w4_plane = zeroed_plane("w4_plane", N)

        load_list("offs2", offs2)
        tab2_w = load_table("tab2_w", tab2_words[0])
        load_scales(tab2_plane, tab2_scales)
        load_wg("wg2", wg2)
        load_weight("w3", w3, 0, 0)
        w2_raw = keep([P, 2 * H], U8, "w2_raw")
        nc.sync.dma_start(w2_raw[:].bitcast(I32), w2_words[0].bitcast(I32))
        load_scales(w2_plane_raw, w2_scales)
        load_coup(0, 0, 1)
        load_page(0, 0)
        load_list("offs4", offs4)
        load_wg("wg1", wg1)
        load_list("offs", offs)
        tab_w = [load_table(f"tab_w{a}", tab_words[a]) for a in range(2)]
        load_scales(tab_plane, tab_scales)
        load_weight("w1", w1, 0, 0)
        load_weight("w1", w1, 1, 0)
        amp_t = load_row_factors("amp_t", amp)
        load_coup(0, 1, 1)
        load_page(0, 1)
        load_list("offs3", offs3)
        load_weight("w3", w3, 0, 1)
        load_list("offs5", offs5)
        load_page(0, 2)
        load_page(0, 3)
        load_weight("w1", w1, 0, 1)
        load_weight("w1", w1, 1, 1)
        load_coup(0, 2, 2)
        gain_t = load_row_factors("gain_t", gain)
        load_page(1, 0)
        load_page(1, 1)
        load_coup(1, 0, 2)
        w4_w = [load_words(keep([P, N], I32, f"w4_w{a}"), w4_words[a]) for a in range(2)]
        load_scales(w4_plane, w4_scales)
        bias_t = keep([P, N_TILES], F32, "bias_t")
        with nc.allow_non_contiguous_dma(reason="one bias value for each output row"):
            nc.sync.dma_start(bias_t[:], bias.rearrange("(n p) -> p n", p=P))
        load_page(1, 2)
        load_page(1, 3)
        load_coup(1, 2, 2)

        def gather_words(name, words, list_name):
            picked = keep([P, S], U32, name)
            nc.vector.tensor_copy(picked[:], words[:].bitcast(U32).indirect(lists[list_name][:]))
            return picked

        def gather_plane(name, plane, list_name):
            picked = keep([P, S], U8, name)
            nc.vector.tensor_copy(picked[:], plane[:].indirect(lists[list_name][:]))
            return picked

        codes, planes = {}, {}

        def quantise_weight(name, a, b, on_scalar):
            rounded = rotating([P, PACK * KP], BF16, "wbf", ROUNDED_BUFS, f"{name}_{a}{b}_bf")
            dst = rounded[:].rearrange("p (t m j) -> p m j t", t=PACK, j=PACK)
            src = raw_weights[name, a, b][:].rearrange("p j (m t) -> p m j t", t=PACK)
            if on_scalar > 0:
                nc.scalar.copy(dst[:, :on_scalar], src[:, :on_scalar])
            if on_scalar < P:
                nc.vector.tensor_copy(dst[:, on_scalar:], src[:, on_scalar:])
            codes[name, a, b] = keep([P, KP], U32, f"{name}_{a}{b}_codes")
            planes[name, a, b] = keep([P, KP], U8, f"{name}_{a}{b}_plane")
            nc.vector.quantize_mx(out=codes[name, a, b][:].bitcast(FP8X4), scales=planes[name, a, b][:], in_=rounded[:])

        v2_w = gather_words("v2_w", tab2_w, "offs2")
        v2_plane = gather_plane("v2_plane", tab2_plane, "offs2")
        quantise_weight("w3", 0, 0, on_scalar=0)

        w2_dealt = keep([P, 2 * H], U8, "w2_dealt")
        w2_plane = keep([P, H], U8, "w2_plane")
        for b in range(2):
            nc.vector.tensor_copy(
                w2_dealt[:, 2 * KP * b : 2 * KP * (b + 1)].rearrange("p (t m e) -> p m t e", t=PACK, e=2),
                w2_raw[:, 2 * KP * b : 2 * KP * (b + 1)].rearrange("p (m t e) -> p m t e", t=PACK, e=2),
            )
            nc.vector.tensor_copy(
                w2_plane[:, KP * b : KP * (b + 1)].rearrange("p (t m) -> p m t", t=PACK),
                w2_plane_raw[:, KP * b : KP * (b + 1)].rearrange("p (m t) -> p m t", t=PACK),
            )

        taken = []

        def next_bank():
            taken.append(banks[4 + len(taken) % 4])
            return taken[-1]

        identity = keep([P, P], F32, "identity")
        make_identity(nc, identity[:])

        def transpose_blocks(bank, src):
            for c in range(BANK // P):
                nc.tensor.transpose(bank[:, P * c : P * (c + 1)], src[:, P * c : P * (c + 1)], identity[:])

        def deal_wg(name):
            turned = next_bank()
            transpose_blocks(turned, wg_rows[name, PACK - 1])
            rows_of_slice = turned[:].rearrange("p (c s t) -> p c t s", c=S // P, t=PACK)
            shape = [P, S // P, P // QUAD, QUAD]
            for t in range(PACK):
                spread = rotating(shape, F32, "got", GOT_BUFS, f"{name}_spread{t}")
                nc.scalar.copy(spread[:], rows_of_slice[:, :, t : t + 1, :].to_broadcast(shape))
                dealt = next_bank()
                transpose_blocks(dealt, spread[:].rearrange("p c q s -> p (c q s)"))
                nc.scalar.copy(wg_rows[name, t], dealt[:])

        def products2(b, t, with_w2, with_w3):
            cols = slice(P * t, P * (t + 1))
            c0 = KP * b + P * t
            nc.tensor.matmul_mx(
                out=with_w2[:], lhsT=w2_dealt[:, 2 * c0 : 2 * (c0 + P)].bitcast(FP4X4), lhsT_scale=w2_plane[:, c0 : c0 + P],
                rhs=v2_w[:].bitcast(FP8X4), rhs_scale=v2_plane[:], start=True, stop=True,
            )
            nc.tensor.matmul_mx(
                out=with_w3[:], lhsT=codes["w3", 0, b][:, cols].bitcast(FP8X4), lhsT_scale=planes["w3", 0, b][:, cols],
                rhs=v2_w[:].bitcast(FP8X4), rhs_scale=v2_plane[:], start=True, stop=True,
            )

        def cosine(b, t, h1):
            cols = slice(P * t, P * (t + 1))
            bank = next_bank()
            for a in range(2):
                nc.tensor.matmul_mx(
                    out=bank[:], lhsT=codes["w1", a, b][:, cols].bitcast(FP8X4), lhsT_scale=planes["w1", a, b][:, cols],
                    rhs=v_w[a][:].bitcast(FP8X4), rhs_scale=v_plane[PACK * a : P, :], start=(a == 0), stop=(a == 1),
                )
            nc.scalar.activation(h1, bank[:], ACT.Sin, scale=0.5)
            nc.scalar.activation(h1, h1, ACT.Square)
            nc.scalar.activation(h1, h1, ACT.Identity, bias=amp_t[:, b, t : t + 1], scale=amp_m2[:, b, t : t + 1])

        def window(b, t, list_name):
            return pages[b, t][:].indirect(lists[list_name][:])

        stream_pairs = {}

        def stream_values(stream, b, t):
            if t % 2 == 0:
                tag, bufs = ("last", LAST_BUFS) if (b, t) == LAST_PAIR else (stream, STREAM_BUFS)
                stream_pairs[stream] = rotating([P, 2, S], F32, tag, bufs, f"{stream}_{b}{t}")
            return stream_pairs[stream][:, t % 2, :]

        def first_pair_stream2(t):
            h2 = stream_values("h2", 0, t)
            with_w2, with_w3 = banks[2 * t], banks[2 * t + 1]
            products2(0, t, with_w2, with_w3)
            nc.vector.tensor_tensor(h2, with_w2[:], coup_rows[0, t], MULT)
            nc.vector.tensor_tensor(h2, with_w3[:], h2, ADD)
            nc.vector.tensor_tensor(window(0, t, "offs4"), h2, wg_rows["wg2", t], MULT)

        def first_pair_stream1(t):
            h1 = stream_values("h1", 0, t)
            cosine(0, t, h1)
            return lambda: nc.vector.tensor_tensor(window(0, t, "offs3"), h1, wg_rows["wg1", t], MULT)

        def stream1(b, t):
            h1 = stream_values("h1", b, t)
            cosine(b, t, h1)
            nc.gpsimd.tensor_tensor(h1, h1, wg_rows["wg1", t], MULT)
            return lambda: nc.vector.tensor_copy(window(b, t, "offs3"), h1)

        def stream2(b, t):
            h2 = stream_values("h2", b, t)
            plain = rotating([P, S], F32, "plain", PLAIN_BUFS, f"plain_{b}{t}")
            with_w2, with_w3 = next_bank(), next_bank()
            products2(b, t, with_w2, with_w3)
            nc.scalar.copy(h2, with_w2[:])
            nc.scalar.copy(plain[:], with_w3[:])
            nc.gpsimd.tensor_tensor(h2, h2, coup_rows[b, t], MULT)
            nc.gpsimd.tensor_tensor(h2, h2, plain[:], ADD)
            if t % 2 == 1:
                nc.gpsimd.tensor_tensor(stream_pairs["h2"][:], stream_pairs["h2"][:], wg_pairs["wg2", t - 1][:], MULT)
            return lambda: nc.vector.tensor_copy(window(b, t, "offs4"), h2)

        def both_streams(b, t0):
            puts1 = [stream1(b, t) for t in (t0, t0 + 1)]
            puts2 = [stream2(b, t) for t in (t0, t0 + 1)]
            return puts1, puts2

        def scatter(puts):
            for put in puts:
                put()

        deal_wg("wg2")
        first_pair_stream2(0)
        deal_wg("wg1")
        v_w = [gather_words(f"v_w{a}", tab_w[a], "offs") for a in range(2)]
        v_plane = gather_plane("v_plane", tab_plane, "offs")
        for a in range(2):
            quantise_weight("w1", a, 0, on_scalar=P // 2)
        amp_m2 = keep([P, 2, PACK], F32, "amp_m2")
        nc.vector.tensor_scalar(amp_m2[:], amp_t[:], -2.0, None, MULT)

        x0_rows = rotating([P, PACK, NP], BF16, "table", TABLE_BUFS, "x0_rows")
        x0_codes = keep([P, NP], U32, "x0_codes")
        x0_plane = keep([P, NP], U8, "x0_plane")
        x1_pairs = rotating([P, 2, NP, 2], BF16, "wraw", RAW_BUFS, "x1_pairs")
        halves = [slice(0, NP // 2), slice(NP // 2, NP)]

        def fetch(b, t, rounded):
            got = rotating([P, NP], F32, "got", GOT_BUFS, f"got{b}{t}")
            nc.vector.tensor_copy(got[:], window(b, t, "offs5"))
            nc.scalar.activation(rounded, got[:], ACT.Copy, scale=gain_t[:, b, t : t + 1])

        def interleave_x0(h):
            woven = rotating([P, PACK * NP // 2], BF16, "table", TABLE_BUFS, f"woven0{h}")
            nc.scalar.copy(
                woven[:].rearrange("p (c l t) -> p c t l", l=LINE, t=PACK),
                x0_rows[:, :, halves[h]].rearrange("p t (c l) -> p c t l", l=LINE),
            )
            return woven

        puts1 = [first_pair_stream1(t) for t in range(2)]
        first_pair_stream2(1)
        scatter(puts1)

        puts1, puts2 = both_streams(0, 2)
        for t in (0, 1):
            fetch(0, t, x0_rows[:, t, :])
        quantise_weight("w3", 0, 1, on_scalar=P)
        scatter(puts1)
        for a in range(2):
            quantise_weight("w1", a, 1, on_scalar=P)
        scatter(puts2)

        puts1, puts2 = both_streams(1, 0)
        for t in (2, 3):
            fetch(0, t, x0_rows[:, t, :])
        woven0 = [interleave_x0(h) for h in range(2)]
        last_puts1, last_puts2 = both_streams(*LAST_PAIR)
        scatter(puts1)
        scatter(puts2)

        for h in range(2):
            nc.vector.quantize_mx(out=x0_codes[:, halves[h]].bitcast(FP8X4), scales=x0_plane[:, halves[h]], in_=woven0[h][:])
            fetch(1, h, x1_pairs[:, 0, :, h])
        scatter(last_puts1)

        free_banks = list(banks)

        def places(width):
            per_bank = BANK // width
            spots = []
            for n in range(N_TILES):
                rank = n % per_bank
                if rank == 0:
                    bank = free_banks.pop(0)
                spots.append((bank[:, width * rank : width * (rank + 1)], rank == 0, rank == per_bank - 1))
            return spots

        def last_product_pass(a, spots, x_codes, x_plane):
            for n, (place, first, last) in enumerate(spots):
                cols = slice(P * n, P * (n + 1))
                nc.tensor.matmul_mx(
                    out=place, lhsT=w4_w[a][:, cols].bitcast(FP8X4), lhsT_scale=w4_plane[PACK * a : P, cols],
                    rhs=x_codes.bitcast(FP8X4), rhs_scale=x_plane, start=(a == 0 and first), stop=(a == 1 and last),
                )

        sums = []
        for c0, width in CHUNKS:
            sums.append(places(width))
            last_product_pass(0, sums[-1], x0_codes[:, c0 : c0 + width], x0_plane[:, c0 : c0 + width])
        scatter(last_puts2)

        out_rows = out.rearrange("(n p) c -> p n c", p=P)
        results = [rotating([P, N_TILES, NP // 2], F32, "wraw", RAW_BUFS, f"result{h}") for h in range(2)]
        got_last, woven1 = {}, {}

        def fetch_chunk(i, u):
            c0, width = CHUNKS[i]
            if u == 0:
                got_last[i] = rotating([P, 2, CHUNK_MAX], F32, "last", LAST_BUFS, f"got_last{i}")
            got = got_last[i][:, u, :width]
            offsets = lists["offs5"][:, c0 // LIST_COL : (c0 + width) // LIST_COL]
            nc.vector.tensor_copy(got, pages[1, 2 + u][:].indirect(offsets))
            nc.scalar.activation(x1_pairs[:, 1, c0 : c0 + width, u], got, ACT.Copy, scale=gain_t[:, 1, 2 + u : 3 + u])

        def interleave_chunk(i):
            c0, width = CHUNKS[i]
            woven1[i] = rotating([P, PACK * CHUNK_MAX], BF16, "woven1", CHUNK_BUFS, f"woven1{i}")[:, : PACK * width]
            words = x1_pairs[:, :, c0 : c0 + width, :].rearrange("p pair c u -> p pair (c u)").bitcast(I32)
            nc.vector.tensor_copy(
                woven1[i].bitcast(I32).rearrange("p (c l pair) -> p c pair l", l=LINE, pair=2),
                words.rearrange("p pair (c l) -> p c pair l", l=LINE),
            )

        def multiply_chunk(i):
            width = CHUNKS[i][1]
            x_codes = rotating([P, CHUNK_MAX], U32, "x1_codes", CHUNK_BUFS, f"x1_codes{i}")
            x_plane = rotating([P, CHUNK_MAX], U8, "x1_plane", CHUNK_BUFS, f"x1_plane{i}")
            nc.vector.quantize_mx(out=x_codes[:, :width].bitcast(FP8X4), scales=x_plane[:, :width], in_=woven1[i])
            last_product_pass(1, sums[i], x_codes[:, :width], x_plane[:, :width])

        def store_chunk(i):
            c0, width = CHUNKS[i]
            start = c0 % (NP // 2)
            result = results[c0 // (NP // 2)][:, :, start : start + width]
            for n, spot in enumerate(sums[i]):
                nc.scalar.activation(result[:, n, :], spot[0], ACT.Abs, bias=bias_t[:, n : n + 1])
            nc.sync.dma_start(out_rows[:, :, c0 : c0 + width], result)

        count = len(CHUNKS)
        for i in range(count + 2):
            if i < count:
                fetch_chunk(i, 0)
            if 1 <= i <= count:
                interleave_chunk(i - 1)
            if i < count:
                fetch_chunk(i, 1)
            if 1 <= i <= count:
                multiply_chunk(i - 1)
            if i >= 2:
                store_chunk(i - 2)
